import numpy as np, ml_dtypes
CORES = [3,11,19,27,35,43,51,59]
N = 8
BF = ml_dtypes.bfloat16
S, SL, W, LN, CAP, T = 2, 2048, 4096, 3, 320, 3
def parts(rng):
    x = rng.integers(0, 256, (N, 8, 16, W)); ga = rng.integers(0, 4, (N, 8, 16, 16)); ha = rng.integers(0, 4, (N, 8, 16, 16))
    w = rng.integers(0, 256, (N, 8, 16)) << rng.integers(0, 5, (N, 8, 16)); od = rng.integers(0, 16, (N, 8))
    np.put_along_axis(w, od[:, :, None], 2 * rng.integers(0, 128, (N, 8, 1)) + 1, 2)
    return x, ga, ha, w, od
def pack(x, ga, ha, w):
    def full(b):
        z = np.zeros((N, 8, 16, 8, 16), np.float32)
        for g in range(8): z[:, g, :, g, :] = b[:, g]
        return z.reshape(N, 128, 128).astype(BF)
    return {"m": np.ascontiguousarray(x.reshape(N, 128, W)).astype(np.float32).astype(BF), "gm": full(ga), "hm": full(ha), "kw": w.reshape(N, 128, 1).astype(np.float32).astype(BF)}
def steer(x, w, i, q, g, cols, who):
    b = x[q, g][:, cols].copy(); b[i] -= b[i] & (N - 1)
    b[i] += (w[q, g, i] * (who - np.dot(w[q, g], b))) & (N - 1)
    x[q, g][:, cols] = b
def nail(x, w, i, k, q, g, cols, goal):
    b = x[q, g][:, cols].copy(); b[i] = 0; b[k] = 0
    v = (goal - np.dot(w[q, g], b)) & 65535; b[i] = v & 255; b[k] = v >> 8
    x[q, g][:, cols] = b
def still(o, q, g, ga, ha, w):
    w[q, g, o[8:]] = 0; ga[q, g][:, o[:8]] = 0; ha[q, g][:, o[:8]] = 0
def setup_inputs(rng):
    x, ga, ha, w, od = parts(rng)
    for q in range(N):
        for g in range(8):
            n = int(rng.integers(0, SL + 1)); steer(x, w, od[q, g], q, g, W - SL + rng.permutation(SL)[:n], int(rng.integers(0, N)))
        g = int(rng.integers(0, 8)); w[q, g] -= w[q, g] & 1
    return pack(x, ga, ha, w)
def setup_inputs_room(rng):
    x, ga, ha, w, od = parts(rng)
    for q in range(N):
        for g in range(8):
            if g % 2 == 0:
                o = rng.permutation(16); od[q, g] = o[0]; w[q, g, o[0]] = 2 * rng.integers(0, 128) + 1; still(o, q, g, ga, ha, w)
            for s in range(S):
                other = (q + 1 + rng.permutation(N - 1)) % N
                if q == 0: other = np.concatenate([np.array([1]), other[other != 1]])
                who = np.full(SL, q); at = 0
                for d in range(N - 1):
                    n = int(rng.choice(np.array([0, 1, CAP - 1, CAP, CAP + 1, CAP, CAP + 1, SL])))
                    if q == 0 and d == 0: n = (CAP, CAP + 1, SL, CAP - 1, CAP + 1, 0, 1, CAP)[g]
                    n = min(n, SL - at); who[at:at + n] = other[d]; at += n
                steer(x, w, od[q, g], q, g, s * SL + rng.permutation(SL), who)
    return pack(x, ga, ha, w)
def setup_inputs_full(rng):
    x, ga, ha, w, od = parts(rng); z = int(rng.integers(0, N)); p = rng.permutation(N)
    for q in range(N):
        for g in range(8):
            o = rng.permutation(16); od[q, g] = o[0]; w[q, g, o[0]] = 2 * rng.integers(0, 128) + 1; still(o, q, g, ga, ha, w)
            for s in range(S):
                if s == S - 1:
                    other = (q + 1 + rng.permutation(N - 1)) % N
                    if q != z: other = np.concatenate([np.array([z]), other[other != z]])
                    who = rng.permutation(np.repeat(other, CAP)[:SL]); who = np.concatenate([who, np.full(SL - len(who), q)])
                elif (p[q] + s) % 2 == 0: who = np.full(SL, q)
                else: who = np.full(SL, (q + int(rng.integers(1, N))) % N)
                steer(x, w, od[q, g], q, g, s * SL + np.arange(SL), who)
    return pack(x, ga, ha, w)
def setup_inputs_alike(rng):
    x, ga, ha, w, od = parts(rng); j = np.arange(SL)
    for q in range(N):
        for g in range(8):
            o = rng.permutation(16); w[q, g, o[0]] = 1; w[q, g, o[1]] = 256
            if g % 2 == 1: still(o, q, g, ga, ha, w)
            for s in range(S):
                cols = s * SL + j; nx = (s + 1) % S
                if g < 2: goal = rng.choice(np.array([0, N * W - 1, q, (W - 1) * N + q, int(rng.integers(0, N * W)), int(rng.integers(0, N * W))]), SL)
                elif g < 4: goal = (nx * SL + np.where(rng.random(SL) < 0.5, j, SL - 1 - j)) * N + np.where(rng.random(SL) < 0.3, q, rng.integers(0, N, SL))
                elif g < 6: goal = (s * SL + j) * N + rng.integers(0, N, SL)
                else: goal = np.full(SL, int(rng.integers(0, W)) * N + (q + 1) % N)
                if g == 6: x[q, g][:, cols] = x[q, g][:, s * SL:s * SL + 1]
                nail(x, w, o[0], o[1], q, g, cols, goal)
    return pack(x, ga, ha, w)
def setup_inputs_ends(rng):
    x, ga, ha, w, od = parts(rng)
    for q in range(N):
        z = rng.permutation(8)
        w[q, z[0]] = 0
        w[q, z[1]] = 4080; x[q, z[1]] = 255; ga[q, z[1]] = 3; ha[q, z[1]] = 3
        x[q, z[2]] = 0
        ga[q, z[3]] = 0; ha[q, z[3]] = 0
        ga[q, z[4]] = 0; ha[q, z[4]] = np.eye(16, dtype=np.int64)
        x[q, z[5]] = 255 * rng.integers(0, 2, (16, W)); ga[q, z[5]] = 3 * rng.integers(0, 2, (16, 16)); ha[q, z[5]] = 3 * rng.integers(0, 2, (16, 16))
        w[q, z[6]] = 0; w[q, z[6], od[q, z[6]]] = 1; ga[q, z[6]] = 3; ha[q, z[6]] = 3
        o = rng.permutation(16); big = o[:14]; g = int(z[7])
        w[q, g, big] = 16 * rng.integers(188, 256, 14); w[q, g, o[14:]] = 2 * rng.integers(0, 128, 2) + 1
        x[q, g] = rng.integers(200, 256, (16, W)); ga[q, g][:, big] = 0; ha[q, g][:, big] = 0
    return pack(x, ga, ha, w)
def setup_inputs_spread(rng):
    x, ga, ha, w, od = parts(rng)
    x = np.minimum((np.exp2(8 * rng.random((N, 8, 1, W))) * rng.random((N, 8, 16, W))).astype(np.int64), 255)
    w = (rng.integers(0, 256, w.shape) >> rng.integers(0, 8, w.shape)) << rng.integers(0, 5, w.shape)
    np.put_along_axis(w, od[:, :, None], 2 * rng.integers(0, 128, (N, 8, 1)) + 1, 2)
    ga = np.where(rng.random(ga.shape) < 0.1 + 0.9 * rng.random((N, 8, 1, 1)), ga, 0); ha = np.where(rng.random(ha.shape) < 0.1 + 0.9 * rng.random((N, 8, 1, 1)), ha, 0)
    return pack(x, ga, ha, w)
def check_inputs(d):
    bad = []
    for k, hi in (("m", 255), ("gm", 3), ("hm", 3), ("kw", 4080)):
        v = np.asarray(d[k]).astype(np.float64)
        if not np.all((v >= 0) & (v <= hi) & (v == np.floor(v))): bad.append("range of " + k)
    p = np.arange(128) >> 4; off = p[:, None] != p[None, :]
    for k in ("gm", "hm"):
        if np.any(np.asarray(d[k]).astype(np.float64)[:, off] != 0): bad.append("blocks of " + k)
    return bad
def reference(m, gm, hm, kw):
    x = m.astype(np.float32).astype(np.int64).reshape(N, 8, 16, W); w = kw.astype(np.float32).astype(np.int64).reshape(N, 8, 16, 1)
    gt = np.swapaxes(gm.astype(np.float64), 1, 2); ht = np.swapaxes(hm.astype(np.float64), 1, 2)
    me = np.eye(N, dtype=bool)[:, None, :, None]; gi = np.arange(8)[None, :, None]
    for t in range(T):
        s = t % S; lo = s * SL; pl = ((s + S - 1) % S) * SL
        prev = x[..., pl:pl + SL]; a = np.add.reduce(prev * w, axis=2)
        who = a & (N - 1); blk = (a >> LN) & (W - 1)
        h = who[:, :, None, :] == np.arange(N)[None, None, :, None]
        cnt = np.add.accumulate(h.astype(np.int64), axis=3)
        ok = np.any(h & ((cnt <= CAP) | me), axis=2)
        ref = np.swapaxes(x[who, gi, :, blk], 2, 3) * ok[:, :, None, :]
        new = np.matmul(gt, prev.reshape(N, 128, SL).astype(np.float64)) + np.matmul(ht, ref.reshape(N, 128, SL).astype(np.float64))
        x[..., lo:lo + SL] = (new.astype(np.int64).reshape(N, 8, 16, SL) + x[..., lo:lo + SL]) & 255
    return {"y": x.reshape(N, 128, W).astype(np.float32).astype(BF)}

@@ -1,0 +1,480 @@
+from concourse.bass import DstId, RemoteDMATransfer
+from concourse.mybir import AluOpType, ActivationFunctionType
+
+N = 8
+SL = 2048
+CAP = 320
+ZCOL = 8 * 4096
+BF = "bfloat16"
+SCRATCH = {"win": ("sbuf", [128, ZCOL + 16], BF), "off": ("sbuf", [128, 128], "uint16")}
+for _n, _w in (("ref", SL), ("qb", SL), ("fin", SL), ("gh", 256), ("kws", 8), ("kwm", 16), ("ps", 384), ("zt", 8 * 144), ("rep", 128),
+               ("ii", 256), ("i256", 128), ("ibp", 128), ("ibn", 128), ("ipm", 128), ("mz", 144), ("tri", 128), ("ta", 128), ("tb", 128),
+               ("c258", 128), ("ones", 512), ("rst", 896), ("hh", 896), ("ss", 896), ("ee", 7 * 144), ("wb", 128), ("qf", 128)):
+    SCRATCH[_n] = ("sbuf", [128, _w], BF)
+for _n, _w in (("hp", 24), ("pc", 24), ("mat", 128), ("matp", 128)):
+    SCRATCH[_n] = ("sbuf", [128, 16, _w], BF)
+for _n, _w in (("ci", 8), ("di", 8), ("dj", 8), ("ai", 128), ("wi", 128), ("ui", 128), ("a3", 128), ("qi", 128)):
+    SCRATCH[_n] = ("sbuf", [128, _w], "int32")
+for _n, _w in (("cf", 16), ("cx", 144), ("m16", 128), ("keym", 128), ("bm", 16), ("df", 8), ("ofs", 8), ("tg", 128)):
+    SCRATCH[_n] = ("sbuf", [128, _w], "float32")
+for _n, _w in (("d0", 8), ("d1", 8), ("hd", 12), ("l0", 8), ("l1", 8)):
+    SCRATCH[_n] = ("dram", [_w, 128, 256], BF)
+for _b in range(8):
+    SCRATCH["pb%d" % _b] = ("psum", [128, 512], "float32")
+
+NDS = 56
+SEMAPHORES = (["cv", "ca", "cp", "cg", "ls", "pa", "r1", "hpar", "hfa", "hfb"] + ["hr%d" % k for k in range(4)]
+              + ["a%d%d" % (s, c) for s in range(2) for c in range(4)] + ["r0%d" % k for k in range(1, 8)]
+              + ["ds%d" % k for k in range(NDS)])
+
+DMA_FIRST = (1, 2, 3)
+DMA_WAVE = {0: ((1, 2, 3, 4), (1, 2, 3, 4), (1, 2, 3), (1, 2)), 1: ((1, 2, 3), (1, 2, 3), (1, 2), (1, 2))}
+BACK1 = {2: (0, 0), 3: (1, 0), 6: (0, 1), 7: (1, 1)}
+BACK0 = {2: (0, 2), 3: (1, 2)}
+FWD0 = ((((2, 3), "hfa"), ((1,), "hfb")), (((4, 5), "hfa"), ((6, 7), "hfb")))
+BANKS = (4, 5, 6, 2, 1)
+
+CY = 0.00104
+PCY = 0.00052
+HOP = 0.1
+LOOK = {"v": 0.25, "a": 0.2, "p": 0.1, "s": 0.0, "g": 0.0}
+
+
+def bits(es):
+    return sum(1 << e for e in es)
+
+
+def hands_of(c, T, topo):
+    far = [d for d in T.cores if topo.chip(d) != topo.chip(c)]
+    return [h for h in topo.cores_of(c) if topo.die(h) != topo.die(c) and all(topo.may_write(h, d) for d in far)][:2]
+
+
+def xfer(topo, dst_core, es, sem, src, dst):
+    rid, pid, _ = topo.addr(dst_core)
+    return RemoteDMATransfer(dst_ids=[DstId(rid=rid, pnc=pid)], dma_engine_mask=bits(es), remote_sem=sem, src=src, dst=dst)
+
+
+def share(es, n, x):
+    w = len(es) // n
+    return es[x * w:(x + 1) * w]
+
+
+def hand_program(g, core, T, topo, me, which):
+    S = T.sem
+    eo = topo.engines(core, T.cores[me ^ 1])
+    sent = 0
+    if which == 0:
+        g.wait_ge(S.hpar, 8)
+        g.remote_dma_fused([xfer(topo, T.cores[me ^ k], eo[k - 1:k], S.pa, T.hp[:, 2 * (me ^ k):2 * (me ^ k) + 2, :],
+                                 T.pc[:, 2 * me:2 * me + 2, :]) for k in range(1, 8)], local_sem=S.ls)
+        sent += 7
+    for ks, sem in FWD0[which]:
+        g.wait_ge(S[sem], 2 * len(ks))
+        g.remote_dma_fused([xfer(topo, T.cores[me ^ k], share(eo, len(ks), x), S["a0%d" % (k // 2)], T.hd[k],
+                                 T.win[:, 256 * me:256 * me + 256]) for x, k in enumerate(ks)], local_sem=S.ls)
+        sent += 8
+    for back, land in ((BACK1, "l1"), (BACK0, "l0")):
+        for k in sorted(back):
+            if back[k][0] == which:
+                x = back[k][1]
+                g.wait_ge(S["hr%d" % x], 4)
+                g.remote_dma_fused([xfer(topo, T.cores[me ^ k], eo, S.r1 if land == "l1" else S["r0%d" % k], T.hd[8 + x],
+                                         T[land][me])], local_sem=S.ls)
+                sent += 8
+    g.wait_ge(S.ls, sent)
+
+
+def overlap(a, b):
+    return a[0] == b[0] and a[1] < b[2] and b[1] < a[2]
+
+
+def lay_out(ops):
+    for n, o in enumerate(ops):
+        deps = set(o["after"])
+        for m in range(n):
+            p = ops[m]
+            if any(overlap(a, b) for a in o["w"] for b in p["r"] + p["w"]) or any(overlap(a, b) for a in o["r"] for b in p["w"]):
+                deps.add(m)
+        o["deps"] = sorted(deps)
+    succ = [[] for _ in ops]
+    for n, o in enumerate(ops):
+        for d in o["deps"]:
+            succ[d].append(n)
+    for n in range(len(ops) - 1, -1, -1):
+        o = ops[n]
+        own = (min(o["eng"].values()) + o["lat"]) if o["eng"] else 0.0
+        o["tail"] = own + max([ops[m]["tail"] + HOP for m in succ[n] if ops[m]["at"] is None] + [0.0])
+    free = {}
+    miss = [len(o["deps"]) for o in ops]
+    ready = []
+    order = []
+
+    def placed(n):
+        for m in succ[n]:
+            miss[m] -= 1
+            if miss[m] == 0 and ops[m]["at"] is None:
+                ready.append(m)
+    for n, o in enumerate(ops):
+        if o["at"] is None and not o["deps"]:
+            ready.append(n)
+    for n, o in enumerate(ops):
+        if o["at"] is not None:
+            o["end"] = o["at"]
+            o["q"] = None
+            placed(n)
+    while ready:
+        cand = []
+        for n in ready:
+            o = ops[n]
+            for q, dur in o["eng"].items():
+                st = free.get(q, 0.0)
+                for d in o["deps"]:
+                    p = ops[d]
+                    if not (q == "p" and p["q"] == "p"):
+                        st = max(st, p["end"] + HOP)
+                cand.append((st + o["pen"] + 0.3 * (dur - min(o["eng"].values())), n, q, st, dur))
+        first = min(cand)
+        near = [c for c in cand if c[2] == first[2] and c[0] <= first[0] + LOOK[first[2]]]
+        _, n, q, st, dur = max(near, key=lambda c: (ops[c[1]]["tail"] + ops[c[1]]["up"] - 2.0 * (c[0] - first[0]), -c[1]))
+        o = ops[n]
+        o["q"] = q
+        o["st"] = st
+        free[q] = st + dur
+        o["end"] = st + dur + o["lat"]
+        ready.remove(n)
+        order.append(n)
+        placed(n)
+    return order
+
+
+def rank_ops(g, core, T, topo, me):
+    S = T.sem
+    A = AluOpType
+    F = ActivationFunctionType
+    ops = []
+    nds = [0]
+    sent = [0]
+    V, P, ACT = g.vector, g.tensor, g.scalar
+    hands = hands_of(core, T, topo)
+    eo = topo.engines(core, T.cores[me ^ 1])
+    ei = [e for e in topo.engines(core, hands[0]) if e not in eo]
+
+    def add(name, eng, fn, r, w, pen=0.0, lat=0.0, after=(), at=None, done=None):
+        ops.append({"name": name, "eng": eng, "fn": fn, "r": list(r), "w": list(w), "pen": pen, "lat": lat, "after": list(after),
+                    "at": at, "done": done, "up": 0.0})
+        return len(ops) - 1
+
+    def K(name, lo=0, hi=1 << 20):
+        return (name, lo, hi)
+
+    def vd(n):
+        return 0.06 + max(64, n) * CY
+
+    def vop(name, n, fn, r, w, pen=0.0):
+        return add(name, {"v": vd(n)}, lambda q: fn(), r, w, pen)
+
+    def either(name, nv, na, fv, fa, r, w, pen=0.0):
+        return add(name, {"v": vd(nv), "a": vd(na)}, lambda q: fv() if q == "v" else fa(), r, w, pen)
+
+    def mm(name, out, bank, lhsT, rhs, n, start, stop, r, pen=0.0):
+        return add(name, {"p": 0.01 + max(64, n) * PCY}, lambda q: P.matmul(out, lhsT, rhs, start, stop), r, [K("pb%d" % bank)], pen, 0.05)
+
+    def dma(name, q, pairs, r, w, lat, pen=0.0):
+        sem = "ds%d" % nds[0]
+        nds[0] += 1
+        Q = {"s": g.sync, "a": g.scalar}[q]
+
+        def fn(_q):
+            for o, i in pairs:
+                Q.dma_start(o, i).then_inc(S[sem], 16)
+        return add(name, {q: 0.08 * len(pairs)}, fn, r, w, pen, lat, done=(sem, 16 * len(pairs)))
+
+    def send(name, trs, cnt, r, after=()):
+        sent[0] += cnt
+        return add(name, {"g": 0.6}, lambda q: g.remote_dma_fused(trs, local_sem=S.ls), r, [], after=after, done=0)
+
+    def arrive(name, sem, cnt, w, at):
+        return add(name, {}, None, [], w, at=at, done=(sem, cnt))
+
+    def ts(out, in0, s1, s2, op0, op1=None):
+        if op1 is None:
+            return V.tensor_scalar(out, in0, s1, None, op0)
+        return V.tensor_scalar(out, in0, s1, s2, op0, op1)
+
+    pb = [T["pb%d" % b] for b in range(8)]
+    win = T.win
+
+    dma("ld_gm", "s", [(T.gh[:, 128:256], T.gm[:]), (T.kws[:, 0:1], T.kw[:])], [], [K("gh", 128, 256), K("kws")], 2.0)
+    dma("ld_hm", "a", [(T.gh[:, 0:128], T.hm[:])], [], [K("gh", 0, 128)], 2.0)
+    for s, lat in ((1, 3.4), (0, 4.6)):
+        d = T["d%d" % s]
+        for x, q in enumerate("sa"):
+            dma("stage%d%s" % (s, q), q, [(d[:, i::16, :], T.m[i::16, s * SL:(s + 1) * SL]) for i in range(x, 16, 2)], [],
+                [K("d%d" % s, x, x + 1)], lat, pen=0.01)
+
+    def gop(name, n, fn, w):
+        return add(name, {"g": 0.16 + 2 * n * CY}, lambda q: fn(), [], w)
+    gop("io_p", 1, lambda: g.iota(T.ci[:, 0:1], [[0, 1]], 0, 1), [K("ci", 0, 1)])
+    gop("io_m16", 128, lambda: g.iota(T.m16[:], [[0, 8], [1, 16]], 0, 0, allow_small_or_imprecise_dtypes=True), [K("m16")])
+    gop("io_cx", 144, lambda: g.iota(T.cx[:], [[1, 144]], 0, 0, allow_small_or_imprecise_dtypes=True), [K("cx")])
+    gop("io_key", 128, lambda: g.iota(T.keym[:], [[2, 8], [32, 8], [1, 2]], 0, 0, allow_small_or_imprecise_dtypes=True), [K("keym")])
+    p0 = T.ci[:, 0:1]
+    for x, (sh, mk) in enumerate(((0, 15), (4, 7), (1, 7), (0, 1))):
+        vop("ci%d" % x, 1, lambda x=x, sh=sh, mk=mk: ts(T.ci[:, x + 1:x + 2], p0, sh, mk, A.arith_shift_right, A.bitwise_and),
+            [K("ci", 0, 1)], [K("ci", x + 1, x + 2)])
+    vop("cf", 5, lambda: V.tensor_copy(T.cf[:, 0:5], T.ci[:, 0:5]), [K("ci")], [K("cf", 0, 5)])
+
+    def col(x):
+        return T.cf[:, x:x + 1]
+    C5 = [K("cf", 0, 5)]
+    CX = [K("cx")]
+    L = 0.3
+    vop("rep", 128, lambda: ts(T.rep[:], T.m16[:], col(1), None, A.is_equal), C5 + [K("m16")], [K("rep")])
+    vop("bm", 16, lambda: ts(T.bm[:], T.cx[:, 0:16], col(2), None, A.is_equal), CX + C5, [K("bm")])
+    vop("kwm", 16, lambda: ts(T.kwm[:], T.bm[:], T.kws[:, 0:1], None, A.mult), [K("bm"), K("kws")], [K("kwm")])
+    for nm, x, a, s1, s2, rd in (("k1", 5, 3, 32.0, col(4), []), ("key", 6, 2, 2.0, col(5), [K("cf", 5, 6)]), ("key16", 7, 6, 1.0, 16.0, [K("cf", 6, 7)]),
+                                 ("iperm", 8, 1, 8.0, col(2), []), ("mzc", 9, 2, 16.0, 15.0, []), ("qcol", 10, 2, -4096.0, 32768.0, [])):
+        vop(nm, 1, lambda x=x, a=a, s1=s1, s2=s2: ts(col(x), col(a), s1, s2, A.mult, A.add), C5 + rd, [K("cf", x, x + 1)], L)
+    vop("ii", 128, lambda: ts(T.ii[:, 0:128], T.cx[:, 0:128], col(0), None, A.is_equal), C5 + CX, [K("ii", 0, 1)], L)
+
+    def aop(name, n, o, sc, bi, w):
+        add(name, {"a": vd(n)}, lambda q: ACT.activation(o, T.ii[:, 0:n], F.Identity, bias=bi, scale=sc), [K("ii", 0, 1 + n // 256)], w)
+    aop("ii2", 128, T.ii[:, 128:256], 1.0, 0.0, [K("ii", 1, 2)])
+    for nm, sc, bi in (("i256", 256.0, 0.0), ("ibp", 32768.0, 0.0), ("ibn", -32768.0, 0.0), ("c258", 0.0, 258.0)):
+        aop(nm, 128, T[nm][:], sc, bi, [K(nm)])
+    for x in range(2):
+        aop("ones", 256, T.ones[:, 256 * x:256 * x + 256], 0.0, 1.0, [K("ones", x, x + 1)])
+    vop("ipm", 128, lambda: ts(T.ipm[:], T.cx[:, 0:128], col(8), None, A.is_equal), CX + [K("cf", 8, 9)], [K("ipm")], L)
+    vop("mz", 144, lambda: ts(T.mz[:], T.cx[:], col(9), None, A.is_equal), CX + [K("cf", 9, 10)], [K("mz")], L)
+    vop("ta", 128, lambda: ts(T.ta[:], T.keym[:], col(6), None, A.is_gt), [K("keym"), K("cf", 6, 7)], [K("ta")], L)
+    vop("tb", 128, lambda: ts(T.tb[:], T.keym[:], col(7), None, A.is_lt), [K("keym"), K("cf", 7, 8)], [K("tb")], L)
+    vop("tri", 256, lambda: V.tensor_tensor(T.tri[:], T.ta[:], T.tb[:], A.mult), [K("ta"), K("tb")], [K("tri")], L)
+    vop("di", 8, lambda: ts(T.di[:], T.cx[:, 0:8], col(3), None, A.add), CX + C5, [K("di")], L)
+    vop("dj", 8, lambda: ts(T.dj[:], T.di[:], 7, None, A.bitwise_and), [K("di")], [K("dj")], L)
+    vop("df", 8, lambda: V.tensor_copy(T.df[:], T.dj[:]), [K("dj")], [K("df")], L)
+    vop("rst", 448, lambda: V.memset(T.rst[:], 1.0), [], [K("rst")], L)
+    vop("rst0", 8, lambda: V.memset(T.rst[:, 0:896:128], 0.0), [], [K("rst")], L)
+    vop("ee", 8, lambda: V.memset(T.ee[:, 15:1008:144], 0.0), [], [K("ee")], L)
+    vop("zero", 16, lambda: V.memset(win[:, ZCOL:ZCOL + 16], 0.0), [], [K("win", ZCOL, ZCOL + 16)], L)
+
+    for d in range(N):
+        mm("pg", pb[0][:, 48 * d:48 * d + 16], 0, T.rep[:], T.gh[:, 128 + 16 * d:144 + 16 * d], 16, True, True, [K("rep"), K("gh")])
+        mm("pw", pb[0][:, 48 * d + 16:48 * d + 24], 0, T.rep[:], T.kwm[:, d:d + 8], 8, True, True, [K("rep"), K("kwm")])
+        mm("ph", pb[0][:, 48 * d + 24:48 * d + 48], 0, T.rep[:], T.gh[:, 16 * d:16 * d + 24], 24, True, True, [K("rep"), K("gh")])
+    vop("ps", 384, lambda: V.tensor_copy(T.ps[:], pb[0][:, 0:384]), [], [K("pb0"), K("ps")])
+    last = send("s_par", [xfer(topo, hands[0], ei, S.hpar, T.ps[:], T.hp[:])], 8, [K("ps")])
+    dma("own_par", "s", [(T.pc[:, 2 * me:2 * me + 2, :], T.ps[:, 48 * me:48 * me + 48])], [K("ps")], [K("pc", 0, 1)], 2.0)
+    arrive("par", "pa", 7, [K("pc", 1, 2)], 9.5)
+
+    def base(s, r, n=256):
+        return win[:, s * SL + 256 * r:s * SL + 256 * r + n]
+
+    def kb(s, r, n=256, q=0):
+        return K("win", q * 4096 + s * SL + 256 * r, q * 4096 + s * SL + 256 * r + n)
+    for ks in ((1,), (2, 3), (4, 5), (6, 7)):
+        last = send("s_1", [xfer(topo, T.cores[me ^ k], share(eo, len(ks), x), S["a1%d" % (k // 2)], T.d1[me ^ k], base(1, me))
+                            for x, k in enumerate(ks)], 8, [K("d1")], [last])
+    for y in range(2):
+        trs = []
+        for h in range(2):
+            ks, sem = FWD0[h][y]
+            for k in ks:
+                trs.append(xfer(topo, hands[h], share(ei, 4, len(trs)), S[sem], T.d0[me ^ k], T.hd[k]))
+        last = send("s_0", trs, 2 * len(trs), [K("d0")], [last])
+    for s in (1, 0):
+        dma("own%d" % s, "s", [(base(s, me), T["d%d" % s][me])], [K("d%d" % s)], [kb(s, me)], 2.2)
+    when = {(1, 0): 6.4, (1, 1): 7.9, (1, 2): 9.5, (1, 3): 11.0, (0, 1): 11.5, (0, 2): 11.6, (0, 0): 13.2, (0, 3): 13.3}
+    for (s, cc), at in when.items():
+        arrive("a%d%d" % (s, cc), "a%d%d" % (s, cc), 8, [kb(s, me ^ k) for k in (2 * cc, 2 * cc + 1) if k], at)
+
+    for r in range(N):
+        vop("z", 65, lambda r=r: ts(T.zt[:, 144 * r:144 * r + 129], T.mz[:, 14 - 2 * r:143 - 2 * r], T.pc[:, 2 * r, 16:17], None, A.mult),
+            [K("mz"), K("pc")], [K("zt", r, r + 1)])
+    for nm, up in (("mat", 5.0), ("matp", 0.0)):
+        for b in range(8):
+            o = T.mat[:, :, 16 * b:16 * b + 16] if nm == "mat" else T.matp[:, :, b::8]
+            either(nm, 128, 256, lambda o=o, b=b: ts(o, T.pc[:, :, 0:16], T.bm[:, b:b + 1], None, A.mult),
+                   lambda o=o, b=b: ACT.activation(o, T.pc[:, :, 0:16], F.Identity, scale=T.bm[:, b:b + 1]),
+                   [K("bm"), K("pc")], [K(nm, b, b + 1)], L)
+            ops[-1]["up"] = up
+
+    rb = [0]
+
+    def turn_pe(s, c, qs):
+        for q in qs:
+            b = BANKS[rb[0] % len(BANKS)]
+            rb[0] += 1
+            mm("rot", pb[b][:], b, T.ii[:, 16 * q:16 * q + 128], base(s, 2 * c, 512), 512, True, True, [K("ii"), kb(s, 2 * c, 512)])
+            o = win[:, q * 4096 + s * SL + 512 * c:q * 4096 + s * SL + 512 * c + 512]
+            either("evac", 512, 512, lambda o=o, b=b: V.tensor_copy(o, pb[b][:]), lambda o=o, b=b: ACT.activation(o, pb[b][:], F.Copy),
+                   [], [K("pb%d" % b), kb(s, 2 * c, 512, q)])
+
+    def turn_dma(s, c, qs, lat):
+        lo = s * SL + 512 * c
+        pairs = []
+        for q in qs:
+            o = q * 4096 + lo
+            pairs.append((win[0:128 - 16 * q, o:o + 512], win[16 * q:128, lo:lo + 512]))
+            pairs.append((win[128 - 16 * q:128, o:o + 512], win[0:16 * q, lo:lo + 512]))
+        dma("turn", "s", pairs, [kb(s, 2 * c, 512)], [kb(s, 2 * c, 512, q) for q in qs], lat)
+
+    def a_part(s, c, first, final):
+        for x in range(4):
+            r, h = 2 * c + x // 2, x % 2
+            lo = s * SL + 256 * r + 128 * h
+            mm("a", pb[7][:, 0:128], 7, T.zt[:, 144 * r + 1 - h:144 * r + 129 - h], win[:, lo:lo + 128], 128, first and x == 0,
+               final and x == 3, [K("zt", r, r + 1), K("win", lo, lo + 128)])
+            ops[-1]["up"] = 2.0
+
+    def index():
+        n0 = len(ops)
+        vop("ai", 128, lambda: V.tensor_copy(T.ai[:], pb[7][:, 0:128]), [], [K("pb7"), K("ai")])
+        vop("wi", 128, lambda: ts(T.wi[:], T.ai[:], 7, None, A.bitwise_and), [K("ai")], [K("wi")])
+        vop("wb", 128, lambda: V.tensor_copy(T.wb[:], T.wi[:]), [K("wi")], [K("wb")])
+        for d in range(7):
+            vop("h", 64, lambda d=d: ts(T.hh[:, 128 * d:128 * d + 128], T.wb[:], T.df[:, d + 1:d + 2], None, A.is_equal),
+                [K("wb"), K("df")], [K("hh", d, d + 1)])
+        vop("scan", 448, lambda: V.tensor_tensor_scan(T.ss[:], T.rst[:], T.hh[:], 0.0, A.mult, A.add), [K("rst"), K("hh")], [K("ss")])
+        mm("off", pb[7][:, 128:135], 7, T.tri[:], T.ss[:, 127:896:128], 7, True, True, [K("tri"), K("ss")])
+        vop("ofs", 8, lambda: ts(T.ofs[:, 0:7], pb[7][:, 128:135], -float(CAP), 0.0, A.add, A.min), [], [K("pb7"), K("ofs")])
+        vop("ui", 128, lambda: ts(T.ui[:], T.ai[:], 3, 0x8FF, A.arith_shift_right, A.bitwise_and), [K("ai")], [K("ui")])
+        vop("a3", 128, lambda: ts(T.a3[:], T.ai[:], 2.0, col(10), A.mult, A.add), [K("ai"), K("cf", 10, 11)], [K("a3")])
+        vop("qi", 128, lambda: ts(T.qi[:], T.a3[:], 0x7000, None, A.bitwise_and), [K("a3")], [K("qi")])
+        vop("qf", 128, lambda: V.tensor_copy(T.qf[:], T.qi[:]), [K("qi")], [K("qf")])
+        fo = pb[3][:, 0:128]
+        mm("f0", fo, 3, T.i256[:], T.wb[:], 128, True, False, [K("i256"), K("wb")])
+        mm("f1", fo, 3, T.ii[:, 0:128], T.qf[:], 128, False, False, [K("ii"), K("qf")])
+        for d in range(7):
+            o = T.ee[:, 144 * d + 16:144 * d + 144]
+            i = T.ss[:, 128 * d:128 * d + 128]
+            ke = K("ee", 144 * d, 144 * d + 144)
+            either("e", 64, 128, lambda o=o, i=i, d=d: ts(o, i, T.ofs[:, d:d + 1], 0.0, A.add, A.max),
+                   lambda o=o, i=i, d=d: ACT.activation(o, i, F.Relu, bias=T.ofs[:, d:d + 1]), [K("ss"), K("ofs")], [ke])
+            mm("fp", fo, 3, T.ibp[:], o, 128, False, False, [K("ibp"), ke])
+            mm("fn", fo, 3, T.ibn[:], T.ee[:, 144 * d + 15:144 * d + 143], 128, False, d == 6, [K("ibn"), ke])
+        vop("tg", 128, lambda: V.tensor_tensor(T.tg[:], fo, T.ui[:], A.add), [K("ui")], [K("pb3"), K("tg")])
+        vop("off", 128, lambda: ts(T.off[:], T.tg[:], float(ZCOL), None, A.min), [K("tg")], [K("off")])
+        for o in ops[n0:]:
+            o["up"] = 3.0
+
+    rest = [q for q in range(1, 8) if q not in DMA_FIRST]
+    for s, cc in sorted(when, key=lambda x: when[x]):
+        c = (me // 2) ^ cc
+        turn_dma(s, c, DMA_FIRST, 3.2)
+        if s == 1:
+            a_part(1, c, cc == 0, cc == 3)
+        if (s, cc) == (1, 3):
+            index()
+        turn_pe(s, c, rest)
+
+    chunks = [(me // 2) ^ cc for cc in (1, 2, 3, 0)]
+
+    def give_back(src, key, land, back, x, after):
+        cc = (1, 2, 3, 0)[x]
+        ks = [k for k in (2 * cc, 2 * cc + 1) if k]
+        near = [k for k in ks if k in back]
+        far = [k for k in ks if k not in back]
+        trs = [xfer(topo, hands[back[k][0]], share(ei, 2, back[k][0]), S["hr%d" % back[k][1]], src(me ^ k), T.hd[8 + back[k][1]]) for k in near]
+        trs += [xfer(topo, T.cores[me ^ k], share(eo, len(far), y), S.r1 if land == "l1" else S["r0%d" % k], src(me ^ k), T[land][me])
+                for y, k in enumerate(far)]
+        return send("back", trs, 4 * len(near) + (8 if far else 0), [key], [after])
+
+    def lands(back, k):
+        return 8 if k in back or (k ^ 1) in back or k == 1 else 4
+
+    for t in range(3):
+        s = t % 2
+        mats = T.matp if t == 2 else T.mat
+        mk = K("matp") if t == 2 else K("mat")
+        unit = T.ipm[:] if t == 2 else T.ii[:, 0:128]
+        for x, c in enumerate(chunks):
+            mm("xc", pb[x][:], x, T.c258[:], T.ones[:], 512, True, False, [K("c258"), K("ones")])
+            mm("xo", pb[x][:], x, unit, base(s, 2 * c, 512), 512, False, False, [K("ii"), K("ipm"), kb(s, 2 * c, 512)])
+            for y in range(2):
+                mm("xg", pb[x][:, 256 * y:256 * y + 256], x, mats[:, 2 * (2 * c + y), :], base(1 - s, 2 * c + y), 256, False, False,
+                   [mk, kb(1 - s, 2 * c + y)])
+        W = win[:, 0:ZCOL + 16]
+        add("gv", {"v": vd(1600)}, lambda q: V.tensor_copy(T.ref[:, 0:1024], W.indirect(T.off[:, 0:64])), [K("win"), K("off")], [K("ref", 0, 1)])
+        add("ga", {"a": vd(1600)}, lambda q: ACT.activation(T.ref[:, 1024:2048], W.indirect(T.off[:, 64:128]), F.Copy),
+            [K("win"), K("off")], [K("ref", 1, 2)])
+        for x, c in enumerate(chunks):
+            for y in range(4):
+                rp = 4 * c + y
+                mm("xh", pb[x][:, 128 * y:128 * y + 128], x, mats[:, 2 * (rp // 2) + 1, :], T.ref[:, rp::16], 128, False, y == 3, [mk, K("ref")])
+        for x, c in enumerate(chunks):
+            qv = T.qb[:, 512 * x:512 * x + 512]
+            add("m1", {"a": vd(512)}, lambda q, x=x, qv=qv: ACT.activation(qv, pb[x][:], F.Identity, bias=-127.5), [], [K("pb%d" % x), K("qb", x, x + 1)])
+            o = T.fin[:, 512 * c:512 * c + 512] if t == 2 else base(s, 2 * c, 512)
+            ko = K("fin", c, c + 1) if t == 2 else kb(s, 2 * c, 512)
+            vop("m2", 512, lambda x=x, qv=qv, o=o: V.tensor_tensor(o, pb[x][:], qv, A.subtract), [K("qb", x, x + 1)], [K("pb%d" % x), ko])
+            if t == 1:
+                last = give_back(lambda r: base(1, r), ko, "l1", BACK1, x, last)
+            if t == 2:
+                last = give_back(lambda r: T.fin[:, 256 * r:256 * r + 256], ko, "l0", BACK0, x, last)
+            else:
+                a_part(s, c, x == 0, x == 3)
+        if t < 2:
+            for x, c in enumerate(chunks):
+                turn_dma(s, c, DMA_WAVE[t][x], 3.0 + 0.5 * x)
+            index()
+            for x, c in enumerate(chunks):
+                turn_pe(s, c, [q for q in range(1, 8) if q not in DMA_WAVE[t][x]])
+        if t == 1:
+            dma("own_l1", "s", [(T.l1[me], base(1, me))], [kb(1, me)], [K("l1", 0, 1)], 2.2, pen=0.5)
+            arrive("r1", "r1", sum(lands(BACK1, k) for k in range(1, 8)), [K("l1", 1, 2)], 0.0)
+            dma("y1", "s", [(T.y[i::16, SL:2 * SL], T.l1[:, i::16, :]) for i in range(16)], [K("l1")], [], 4.0, pen=1.0)
+    dma("y_own", "a", [(T.y[16 * me:16 * me + 16, 0:SL], T.fin[:, 256 * me:256 * me + 256])], [K("fin")], [], 2.0)
+    for x, k in enumerate((4, 5, 6, 7, 2, 3, 1)):
+        arrive("r0", "r0%d" % k, lands(BACK0, k), [K("l0", k, k + 1)], 0.0)
+        dma("y0", "sa"[x % 2], [(T.y[16 * (me ^ k):16 * (me ^ k) + 16, 0:SL], T.l0[me ^ k])], [K("l0", k, k + 1), K("fin")], [], 2.0,
+            pen=0.1 + 0.01 * x)
+    return ops, sent[0]
+
+
+def rank_program(g, core, T, topo):
+    me = T.rank_of(core)
+    if me is None:
+        for c in topo.cores_of(core):
+            r = T.rank_of(c)
+            if r is not None and core in hands_of(c, T, topo):
+                hand_program(g, core, T, topo, r, hands_of(c, T, topo).index(core))
+        return
+    ops, sent = rank_ops(g, core, T, topo, me)
+    order = lay_out(ops)
+    Q = {"v": g.vector, "a": g.scalar, "p": g.tensor, "s": g.sync, "g": g}
+    need = set()
+    for n in order:
+        for d in ops[n]["deps"]:
+            if not (ops[n]["q"] == "p" and ops[d]["q"] == "p"):
+                need.add(d)
+    cnt = {}
+    seen = {q: {} for q in Q}
+    total = {}
+    for n in order:
+        o = ops[n]
+        q = o["q"]
+        want = {}
+        for d in o["deps"]:
+            p = ops[d]
+            if p["done"] == 0 or (q == "p" and p["q"] == "p"):
+                continue
+            sem, val = p["done"]
+            want[sem] = max(want.get(sem, 0), val)
+        for sem, val in want.items():
+            if seen[q].get(sem, 0) < val:
+                Q[q].wait_ge(T.sem[sem], val)
+                seen[q][sem] = val
+        ins = o["fn"](q)
+        if o["done"] is None:
+            if n in need:
+                cnt[q] = cnt.get(q, 0) + 1
+                o["done"] = ("c" + q, cnt[q])
+                ins.then_inc(T.sem["c" + q], 1)
+            else:
+                o["done"] = 0
+        if o["done"] != 0:
+            total[o["done"][0]] = o["done"][1]
+    for sem, val in total.items():
+        if not any(seen[q].get(sem, 0) >= val for q in Q):
+            g.wait_ge(T.sem[sem], val)
+    g.wait_ge(T.sem.ls, sent)

@@ -27,11 +27,15 @@ SEMAPHORES = (["cv", "ca", "cp", "cg", "ls", "pa", "r1", "hpar", "hfa", "hfb"] +
               + ["a%d%d" % (s, c) for s in range(2) for c in range(4)] + ["r0%d" % k for k in range(1, 8)]
               + ["ds%d" % k for k in range(NDS)])
 
-DMA_FIRST = (1, 2, 3)
-DMA_WAVE = {0: ((1, 2, 3, 4), (1, 2, 3, 4), (1, 2, 3), (1, 2)), 1: ((1, 2, 3), (1, 2, 3), (1, 2), (1, 2))}
-BACK1 = {2: (0, 0), 3: (1, 0), 6: (0, 1), 7: (1, 1)}
-BACK0 = {2: (0, 2), 3: (1, 2)}
-FWD0 = ((((2, 3), "hfa"), ((1,), "hfb")), (((4, 5), "hfa"), ((6, 7), "hfb")))
+WORK = (2, 3, 1, 0)
+DMA_FIRST = ((1, (0,), (1, 2, 3)), (1, (1,), (1, 2, 3)), (1, (2,), (1, 2, 3)), (1, (3,), (1, 2, 3)), (0, (2, 3), (1, 2, 3, 4)),
+             (0, (0, 1), (1, 2, 3, 4)))
+DMA_WAVE = {0: (((2,), (1, 2)), ((3,), (1, 2)), ((2, 3), (3, 4, 5)), ((0, 1), (1, 2, 3))),
+            1: (((2,), (1, 2)), ((3,), (1, 2)), ((2, 3), (3, 4)), ((0, 1), (1, 2)))}
+BACK1 = {4: (0, 0), 5: (1, 0), 2: (0, 1), 3: (1, 1)}
+BACK0 = {4: (0, 2), 5: (1, 2)}
+STORE0 = (6, 7, 2, 3, 4, 5, 1)
+FWD0 = ((((4, 5), "hfa"), ((1,), "hfb")), (((6, 7), "hfa"), ((2, 3), "hfb")))
 BANKS = (4, 5, 6, 2, 1)
 
 CY = 0.00104
@@ -74,7 +78,7 @@ def hand_program(g, core, T, topo, me, which):
                                  T.win[:, 256 * me:256 * me + 256]) for x, k in enumerate(ks)], local_sem=S.ls)
         sent += 8
     for back, land in ((BACK1, "l1"), (BACK0, "l0")):
-        for k in sorted(back):
+        for k in back:
             if back[k][0] == which:
                 x = back[k][1]
                 g.wait_ge(S["hr%d" % x], 4)
@@ -283,7 +287,7 @@ def rank_ops(g, core, T, topo, me):
         last = send("s_0", trs, 2 * len(trs), [K("d0")], [last])
     for s in (1, 0):
         dma("own%d" % s, "s", [(base(s, me), T["d%d" % s][me])], [K("d%d" % s)], [kb(s, me)], 2.2)
-    when = {(1, 0): 6.4, (1, 1): 7.9, (1, 2): 9.5, (1, 3): 11.0, (0, 1): 11.5, (0, 2): 11.6, (0, 0): 13.2, (0, 3): 13.3}
+    when = {(1, 0): 6.4, (1, 1): 7.9, (1, 2): 9.5, (1, 3): 11.0, (0, 2): 11.5, (0, 3): 11.6, (0, 0): 13.2, (0, 1): 13.3}
     for (s, cc), at in when.items():
         arrive("a%d%d" % (s, cc), "a%d%d" % (s, cc), 8, [kb(s, me ^ k) for k in (2 * cc, 2 * cc + 1) if k], at)
 
@@ -300,8 +304,14 @@ def rank_ops(g, core, T, topo, me):
 
     rb = [0]
 
-    def turn_pe(s, c, qs):
-        for q in qs:
+    def place(cc):
+        return (me // 2) ^ cc
+
+    def turn_pe(s, cc, by_dma):
+        c = place(cc)
+        for q in range(1, 8):
+            if any(cc in ccs and q in qs for ccs, qs in by_dma):
+                continue
             b = BANKS[rb[0] % len(BANKS)]
             rb[0] += 1
             mm("rot", pb[b][:], b, T.ii[:, 16 * q:16 * q + 128], base(s, 2 * c, 512), 512, True, True, [K("ii"), kb(s, 2 * c, 512)])
@@ -309,14 +319,16 @@ def rank_ops(g, core, T, topo, me):
             either("evac", 512, 512, lambda o=o, b=b: V.tensor_copy(o, pb[b][:]), lambda o=o, b=b: ACT.activation(o, pb[b][:], F.Copy),
                    [], [K("pb%d" % b), kb(s, 2 * c, 512, q)])
 
-    def turn_dma(s, c, qs, lat):
+    def turn_dma(s, ccs, qs, lat):
+        c = min(place(cc) for cc in ccs)
+        n = 512 * len(ccs)
         lo = s * SL + 512 * c
         pairs = []
         for q in qs:
             o = q * 4096 + lo
-            pairs.append((win[0:128 - 16 * q, o:o + 512], win[16 * q:128, lo:lo + 512]))
-            pairs.append((win[128 - 16 * q:128, o:o + 512], win[0:16 * q, lo:lo + 512]))
-        dma("turn", "s", pairs, [kb(s, 2 * c, 512)], [kb(s, 2 * c, 512, q) for q in qs], lat)
+            pairs.append((win[0:128 - 16 * q, o:o + n], win[16 * q:128, lo:lo + n]))
+            pairs.append((win[128 - 16 * q:128, o:o + n], win[0:16 * q, lo:lo + n]))
+        dma("turn", "s", pairs, [kb(s, 2 * c, n)], [kb(s, 2 * c, n, q) for q in qs], lat)
 
     def a_part(s, c, first, final):
         for x in range(4):
@@ -357,20 +369,19 @@ def rank_ops(g, core, T, topo, me):
         for o in ops[n0:]:
             o["up"] = 3.0
 
-    rest = [q for q in range(1, 8) if q not in DMA_FIRST]
+    for s, ccs, qs in DMA_FIRST:
+        turn_dma(s, ccs, qs, 3.2 * len(ccs))
     for s, cc in sorted(when, key=lambda x: when[x]):
-        c = (me // 2) ^ cc
-        turn_dma(s, c, DMA_FIRST, 3.2)
         if s == 1:
-            a_part(1, c, cc == 0, cc == 3)
+            a_part(1, place(cc), cc == 0, cc == 3)
         if (s, cc) == (1, 3):
             index()
-        turn_pe(s, c, rest)
+        turn_pe(s, cc, [(ccs, qs) for z, ccs, qs in DMA_FIRST if z == s])
 
-    chunks = [(me // 2) ^ cc for cc in (1, 2, 3, 0)]
+    chunks = [place(cc) for cc in WORK]
 
     def give_back(src, key, land, back, x, after):
-        cc = (1, 2, 3, 0)[x]
+        cc = WORK[x]
         ks = [k for k in (2 * cc, 2 * cc + 1) if k]
         near = [k for k in ks if k in back]
         far = [k for k in ks if k not in back]
@@ -403,7 +414,11 @@ def rank_ops(g, core, T, topo, me):
                 mm("xh", pb[x][:, 128 * y:128 * y + 128], x, mats[:, 2 * (rp // 2) + 1, :], T.ref[:, rp::16], 128, False, y == 3, [mk, K("ref")])
         for x, c in enumerate(chunks):
             qv = T.qb[:, 512 * x:512 * x + 512]
-            add("m1", {"a": vd(512)}, lambda q, x=x, qv=qv: ACT.activation(qv, pb[x][:], F.Identity, bias=-127.5), [], [K("pb%d" % x), K("qb", x, x + 1)])
+            if x == 0 and t < 2:
+                vop("m1", 512, lambda x=x, qv=qv: ts(qv, pb[x][:], -127.5, None, A.add), [], [K("pb%d" % x), K("qb", x, x + 1)])
+            else:
+                add("m1", {"a": vd(512)}, lambda q, x=x, qv=qv: ACT.activation(qv, pb[x][:], F.Identity, bias=-127.5), [],
+                    [K("pb%d" % x), K("qb", x, x + 1)])
             o = T.fin[:, 512 * c:512 * c + 512] if t == 2 else base(s, 2 * c, 512)
             ko = K("fin", c, c + 1) if t == 2 else kb(s, 2 * c, 512)
             vop("m2", 512, lambda x=x, qv=qv, o=o: V.tensor_tensor(o, pb[x][:], qv, A.subtract), [K("qb", x, x + 1)], [K("pb%d" % x), ko])
@@ -414,17 +429,17 @@ def rank_ops(g, core, T, topo, me):
             else:
                 a_part(s, c, x == 0, x == 3)
         if t < 2:
-            for x, c in enumerate(chunks):
-                turn_dma(s, c, DMA_WAVE[t][x], 3.0 + 0.5 * x)
+            for x, (ccs, qs) in enumerate(DMA_WAVE[t]):
+                turn_dma(s, ccs, qs, 3.0 + 0.7 * x)
             index()
-            for x, c in enumerate(chunks):
-                turn_pe(s, c, [q for q in range(1, 8) if q not in DMA_WAVE[t][x]])
+            for cc in WORK:
+                turn_pe(s, cc, DMA_WAVE[t])
         if t == 1:
             dma("own_l1", "s", [(T.l1[me], base(1, me))], [kb(1, me)], [K("l1", 0, 1)], 2.2, pen=0.5)
             arrive("r1", "r1", sum(lands(BACK1, k) for k in range(1, 8)), [K("l1", 1, 2)], 0.0)
             dma("y1", "s", [(T.y[i::16, SL:2 * SL], T.l1[:, i::16, :]) for i in range(16)], [K("l1")], [], 4.0, pen=1.0)
     dma("y_own", "a", [(T.y[16 * me:16 * me + 16, 0:SL], T.fin[:, 256 * me:256 * me + 256])], [K("fin")], [], 2.0)
-    for x, k in enumerate((4, 5, 6, 7, 2, 3, 1)):
+    for x, k in enumerate(STORE0):
         arrive("r0", "r0%d" % k, lands(BACK0, k), [K("l0", k, k + 1)], 0.0)
         dma("y0", "sa"[x % 2], [(T.y[16 * (me ^ k):16 * (me ^ k) + 16, 0:SL], T.l0[me ^ k])], [K("l0", k, k + 1), K("fin")], [], 2.0,
             pen=0.1 + 0.01 * x)

@@ -4,18 +4,26 @@ from concourse.mybir import AluOpType, ActivationFunctionType
 N = 8
 SL = 2048
 CAP = 320
-ZCOL = 8 * 4096
+GAP = 128
+START = (GAP, 2 * GAP + 4 * SL, 3 * GAP + 12 * SL, 4 * GAP + 20 * SL, 5 * GAP + 28 * SL)
+LISTS = (2, 1, 1)
+RW = 128
+SEG = RW + 1
 BF = "bfloat16"
-SCRATCH = {"win": ("sbuf", [128, ZCOL + 16], BF), "off": ("sbuf", [128, 128], "uint16")}
-for _n, _w in (("ref", SL), ("qb", SL), ("fin", SL), ("gh", 256), ("kws", 8), ("kwm", 16), ("ps", 384), ("zt", 8 * 144), ("rep", 128),
-               ("ii", 256), ("i256", 128), ("ibp", 128), ("ibn", 128), ("ipm", 128), ("mz", 144), ("tri", 128), ("ta", 128), ("tb", 128),
-               ("c258", 128), ("ones", 512), ("rst", 896), ("hh", 896), ("ss", 896), ("ee", 7 * 144), ("wb", 128), ("qf", 128)):
+SCRATCH = {"win": ("sbuf", [128, START[4]], BF), "off": ("sbuf", [128, 256], "uint16")}
+UNITS = (("ibp", 65536.0), ("ibn", -65536.0), ("im1", -1.0), ("i2k", 2048.0), ("im2k", -2048.0), ("i18", 1792.0),
+         ("is0", float(START[1] - START[0])), ("is1", float(START[1] - START[2])), ("is2", float(START[3] - START[2])),
+         ("i24", 24576.0), ("im16", -16384.0))
+for _n, _w in (("ref", 2 * SL), ("qb", SL), ("fin", SL), ("gh", 256), ("kws", 8), ("kwm", 16), ("ps", 384), ("zt", 8 * 144), ("rep", 128),
+               ("ii", 256), ("ipm", 128), ("mz", 144), ("tri", 128), ("ta", 128), ("tb", 128), ("dq", 128), ("cst", 128), ("c25", 128),
+               ("c258", 128), ("ones", 512), ("top", 912), ("hh", 912), ("ss", 912), ("lid", 912), ("cc", 912), ("wb", 128), ("r15", 128),
+               ("hs", 128), ("lt", 128), ("k11", 128), ("k14", 128), ("k13c", 128), ("k14c", 128)) + tuple((u[0], 128) for u in UNITS):
     SCRATCH[_n] = ("sbuf", [128, _w], BF)
-for _n, _w in (("hp", 24), ("pc", 24), ("mat", 128), ("matp", 128)):
+for _n, _w in (("hp", 24), ("pc", 24), ("mat", 192), ("matp", 128)):
     SCRATCH[_n] = ("sbuf", [128, 16, _w], BF)
-for _n, _w in (("ci", 8), ("di", 8), ("dj", 8), ("ai", 128), ("wi", 128), ("ui", 128), ("a3", 128), ("qi", 128)):
+for _n, _w in (("ci", 8), ("di", 8), ("dj", 8)):
     SCRATCH[_n] = ("sbuf", [128, _w], "int32")
-for _n, _w in (("cf", 16), ("cx", 144), ("m16", 128), ("keym", 128), ("bm", 16), ("df", 8), ("ofs", 8), ("tg", 128)):
+for _n, _w in (("cf", 16), ("cx", 144), ("m16", 128), ("keym", 128), ("bm", 16), ("df", 8), ("r3", 128), ("yy", 128), ("i32", 128)):
     SCRATCH[_n] = ("sbuf", [128, _w], "float32")
 for _n, _w in (("d0", 8), ("d1", 8), ("hd", 12), ("l0", 8), ("l1", 8)):
     SCRATCH[_n] = ("dram", [_w, 128, 256], BF)
@@ -28,20 +36,29 @@ SEMAPHORES = (["cv", "ca", "cp", "cg", "ls", "pa", "r1", "hpar", "hfa", "hfb"] +
               + ["ds%d" % k for k in range(NDS)])
 
 WORK = (2, 3, 1, 0)
-DMA_FIRST = ((1, (0,), (1, 2, 3)), (1, (1,), (1, 2, 3)), (1, (2,), (1, 2, 3)), (1, (3,), (1, 2, 3)), (0, (2, 3), (1, 2, 3, 4)),
-             (0, (0, 1), (1, 2, 3, 4)))
-DMA_WAVE = {0: (((2,), (1, 2)), ((3,), (1, 2)), ((2, 3), (3, 4, 5)), ((0, 1), (1, 2, 3))),
-            1: (((2,), (1, 2)), ((3,), (1, 2)), ((2, 3), (3, 4)), ((0, 1), (1, 2)))}
+BY_DMA = {0: (((2, 3), (1, 2, 3)), ((0, 1), (1,))), 1: (),
+          2: (((2,), (1, 2)), ((3,), (1, 2)), ((2, 3), (3, 5, 6)), ((0, 1), (1, 2, 3))),
+          3: (((2,), (1, 2)), ((3,), (1, 2)), ((2, 3), (3, 5)), ((0, 1), (1, 2, 3)))}
+LATE = (((0, 1), (5, 6, 7)), ((2, 3), (5, 6, 7)))
+BY_POOL = {0: (), 1: (0, 1, 2, 3), 2: (2, 3), 3: (2, 3)}
 BACK1 = {4: (0, 0), 5: (1, 0), 2: (0, 1), 3: (1, 1)}
 BACK0 = {4: (0, 2), 5: (1, 2)}
 STORE0 = (6, 7, 2, 3, 4, 5, 1)
+OUT1 = ((1,), (2, 3), (4, 5), (6, 7))
 FWD0 = ((((4, 5), "hfa"), ((1,), "hfb")), (((6, 7), "hfa"), ((2, 3), "hfb")))
-BANKS = (4, 5, 6, 2, 1)
+BANKS = ((4, 5, 1, 3), (4, 5, 7, 3, 2))
+
+BIG1 = 1.5 * 2 ** 23
+BIG4096 = 1.5 * 2 ** 35
+SHIFT = (-2.0 ** 20, 14336.0, 0.0625)
+KO = 130
 
 CY = 0.00104
 PCY = 0.00052
 HOP = 0.1
+UNIT = 0.33
 LOOK = {"v": 0.25, "a": 0.2, "p": 0.1, "s": 0.0, "g": 0.0}
+UP = {"rot": 6.0, "evac": 2.0, "a": 8.0, "index": 3.0, "wave": 6.0, "mat": 8.0, "matp": -3.0, "x": 0.0}
 
 
 def bits(es):
@@ -75,7 +92,7 @@ def hand_program(g, core, T, topo, me, which):
     for ks, sem in FWD0[which]:
         g.wait_ge(S[sem], 2 * len(ks))
         g.remote_dma_fused([xfer(topo, T.cores[me ^ k], share(eo, len(ks), x), S["a0%d" % (k // 2)], T.hd[k],
-                                 T.win[:, 256 * me:256 * me + 256]) for x, k in enumerate(ks)], local_sem=S.ls)
+                                 T.win[:, START[0] + 256 * me:START[0] + 256 * me + 256]) for x, k in enumerate(ks)], local_sem=S.ls)
         sent += 8
     for back, land in ((BACK1, "l1"), (BACK0, "l0")):
         for k in back:
@@ -92,26 +109,36 @@ def overlap(a, b):
     return a[0] == b[0] and a[1] < b[2] and b[1] < a[2]
 
 
+def waits(o, d, p, q):
+    return not (p["q"] == q and (d in o["soft"] or d in o["after"]))
+
+
 def lay_out(ops):
     for n, o in enumerate(ops):
         deps = set(o["after"])
+        soft = set()
         for m in range(n):
             p = ops[m]
-            if any(overlap(a, b) for a in o["w"] for b in p["r"] + p["w"]) or any(overlap(a, b) for a in o["r"] for b in p["w"]):
+            met = [a for a in o["w"] for b in p["r"] + p["w"] if overlap(a, b)] + [a for a in o["r"] for b in p["w"] if overlap(a, b)]
+            if met:
                 deps.add(m)
+                if all(a[0].startswith("pb") for a in met):
+                    soft.add(m)
         o["deps"] = sorted(deps)
+        o["soft"] = soft
     succ = [[] for _ in ops]
     for n, o in enumerate(ops):
         for d in o["deps"]:
             succ[d].append(n)
     for n in range(len(ops) - 1, -1, -1):
         o = ops[n]
-        own = (min(o["eng"].values()) + o["lat"]) if o["eng"] else 0.0
+        own = (min(o["eng"].values()) + o["lat"] + o["work"]) if o["eng"] else 0.0
         o["tail"] = own + max([ops[m]["tail"] + HOP for m in succ[n] if ops[m]["at"] is None] + [0.0])
     free = {}
     miss = [len(o["deps"]) for o in ops]
     ready = []
     order = []
+    busy = [0]
 
     def placed(n):
         for m in succ[n]:
@@ -131,11 +158,12 @@ def lay_out(ops):
         for n in ready:
             o = ops[n]
             for q, dur in o["eng"].items():
+                if q == "v" and busy[0] and len(o["eng"]) > 1:
+                    continue
                 st = free.get(q, 0.0)
                 for d in o["deps"]:
-                    p = ops[d]
-                    if not (q == "p" and p["q"] == "p"):
-                        st = max(st, p["end"] + HOP)
+                    if waits(o, d, ops[d], q):
+                        st = max(st, ops[d]["end"] + HOP)
                 cand.append((st + o["pen"] + 0.3 * (dur - min(o["eng"].values())), n, q, st, dur))
         first = min(cand)
         near = [c for c in cand if c[2] == first[2] and c[0] <= first[0] + LOOK[first[2]]]
@@ -145,7 +173,10 @@ def lay_out(ops):
         o["st"] = st
         free[q] = st + dur
         o["end"] = st + dur + o["lat"]
+        if o["work"]:
+            o["end"] = free["dma"] = max(o["end"], free.get("dma", 0.0)) + o["work"]
         ready.remove(n)
+        busy[0] += {"r3": 1, "scan2": -0.5}.get(o["name"], 0)
         order.append(n)
         placed(n)
     return order
@@ -163,10 +194,14 @@ def rank_ops(g, core, T, topo, me):
     eo = topo.engines(core, T.cores[me ^ 1])
     ei = [e for e in topo.engines(core, hands[0]) if e not in eo]
 
-    def add(name, eng, fn, r, w, pen=0.0, lat=0.0, after=(), at=None, done=None):
+    def add(name, eng, fn, r, w, pen=0.0, lat=0.0, after=(), at=None, done=None, work=0.0):
         ops.append({"name": name, "eng": eng, "fn": fn, "r": list(r), "w": list(w), "pen": pen, "lat": lat, "after": list(after),
-                    "at": at, "done": done, "up": 0.0})
+                    "at": at, "done": done, "up": 0.0, "work": work})
         return len(ops) - 1
+
+    def rise(n0, up):
+        for o in ops[n0:]:
+            o["up"] = up
 
     def K(name, lo=0, hi=1 << 20):
         return (name, lo, hi)
@@ -183,7 +218,7 @@ def rank_ops(g, core, T, topo, me):
     def mm(name, out, bank, lhsT, rhs, n, start, stop, r, pen=0.0):
         return add(name, {"p": 0.01 + max(64, n) * PCY}, lambda q: P.matmul(out, lhsT, rhs, start, stop), r, [K("pb%d" % bank)], pen, 0.05)
 
-    def dma(name, q, pairs, r, w, lat, pen=0.0):
+    def dma(name, q, pairs, r, w, lat, pen=0.0, work=0.0, after=()):
         sem = "ds%d" % nds[0]
         nds[0] += 1
         Q = {"s": g.sync, "a": g.scalar}[q]
@@ -191,11 +226,13 @@ def rank_ops(g, core, T, topo, me):
         def fn(_q):
             for o, i in pairs:
                 Q.dma_start(o, i).then_inc(S[sem], 16)
-        return add(name, {q: 0.08 * len(pairs)}, fn, r, w, pen, lat, done=(sem, 16 * len(pairs)))
+        return add(name, {q: 0.08 * len(pairs)}, fn, r, w, pen, lat, done=(sem, 16 * len(pairs)), work=work, after=after)
 
-    def send(name, trs, cnt, r, after=()):
+    def send(name, trs, cnt, r, after=(), work=0.0):
         sent[0] += cnt
-        return add(name, {"g": 0.6}, lambda q: g.remote_dma_fused(trs, local_sem=S.ls), r, [], after=after, done=0)
+        n = add(name, {"g": 0.6}, lambda q: g.remote_dma_fused(trs, local_sem=S.ls), r, [], after=after, done=0, work=work)
+        ops[n]["up"] = 30.0
+        return n
 
     def arrive(name, sem, cnt, w, at):
         return add(name, {}, None, [], w, at=at, done=(sem, cnt))
@@ -216,12 +253,12 @@ def rank_ops(g, core, T, topo, me):
             dma("stage%d%s" % (s, q), q, [(d[:, i::16, :], T.m[i::16, s * SL:(s + 1) * SL]) for i in range(x, 16, 2)], [],
                 [K("d%d" % s, x, x + 1)], lat, pen=0.01)
 
-    def gop(name, n, fn, w):
-        return add(name, {"g": 0.16 + 2 * n * CY}, lambda q: fn(), [], w)
+    def gop(name, n, fn, w, r=()):
+        return add(name, {"g": 0.16 + 2 * n * CY}, lambda q: fn(), r, w)
     gop("io_p", 1, lambda: g.iota(T.ci[:, 0:1], [[0, 1]], 0, 1), [K("ci", 0, 1)])
     gop("io_m16", 128, lambda: g.iota(T.m16[:], [[0, 8], [1, 16]], 0, 0, allow_small_or_imprecise_dtypes=True), [K("m16")])
     gop("io_cx", 144, lambda: g.iota(T.cx[:], [[1, 144]], 0, 0, allow_small_or_imprecise_dtypes=True), [K("cx")])
-    gop("io_key", 128, lambda: g.iota(T.keym[:], [[2, 8], [32, 8], [1, 2]], 0, 0, allow_small_or_imprecise_dtypes=True), [K("keym")])
+    gop("io_key", 128, lambda: g.iota(T.keym[:], [[2, 8], [64, 8], [1, 2]], 0, 0, allow_small_or_imprecise_dtypes=True), [K("keym")])
     p0 = T.ci[:, 0:1]
     for x, (sh, mk) in enumerate(((0, 15), (4, 7), (1, 7), (0, 1))):
         vop("ci%d" % x, 1, lambda x=x, sh=sh, mk=mk: ts(T.ci[:, x + 1:x + 2], p0, sh, mk, A.arith_shift_right, A.bitwise_and),
@@ -236,16 +273,23 @@ def rank_ops(g, core, T, topo, me):
     vop("rep", 128, lambda: ts(T.rep[:], T.m16[:], col(1), None, A.is_equal), C5 + [K("m16")], [K("rep")])
     vop("bm", 16, lambda: ts(T.bm[:], T.cx[:, 0:16], col(2), None, A.is_equal), CX + C5, [K("bm")])
     vop("kwm", 16, lambda: ts(T.kwm[:], T.bm[:], T.kws[:, 0:1], None, A.mult), [K("bm"), K("kws")], [K("kwm")])
-    for nm, x, a, s1, s2, rd in (("k1", 5, 3, 32.0, col(4), []), ("key", 6, 2, 2.0, col(5), [K("cf", 5, 6)]), ("key16", 7, 6, 1.0, 16.0, [K("cf", 6, 7)]),
-                                 ("iperm", 8, 1, 8.0, col(2), []), ("mzc", 9, 2, 16.0, 15.0, []), ("qcol", 10, 2, -4096.0, 32768.0, [])):
+    rise(0, 60.0)
+    n0 = len(ops)
+    for nm, x, a, s1, s2, rd in (("k1", 5, 3, 64.0, col(4), []), ("key", 6, 2, 2.0, col(5), [K("cf", 5, 6)]),
+                                 ("key32", 7, 6, 1.0, 32.0, [K("cf", 6, 7)]), ("iperm", 8, 1, 8.0, col(2), []),
+                                 ("mzc", 9, 2, 16.0, 15.0, []), ("qcol", 10, 2, -2048.0, 16384.0, []), ("q14", 13, 2, -0.125, KO + 1.5, []),
+                                 ("q13", 14, 2, -0.25, KO + 3.5, [])):
         vop(nm, 1, lambda x=x, a=a, s1=s1, s2=s2: ts(col(x), col(a), s1, s2, A.mult, A.add), C5 + rd, [K("cf", x, x + 1)], L)
     vop("ii", 128, lambda: ts(T.ii[:, 0:128], T.cx[:, 0:128], col(0), None, A.is_equal), C5 + CX, [K("ii", 0, 1)], L)
 
-    def aop(name, n, o, sc, bi, w):
-        add(name, {"a": vd(n)}, lambda q: ACT.activation(o, T.ii[:, 0:n], F.Identity, bias=bi, scale=sc), [K("ii", 0, 1 + n // 256)], w)
+    def aop(name, n, o, sc, bi, w, r=()):
+        add(name, {"a": vd(n)}, lambda q: ACT.activation(o, T.ii[:, 0:n], F.Identity, bias=bi, scale=sc), [K("ii", 0, 1 + n // 256)] + list(r), w)
     aop("ii2", 128, T.ii[:, 128:256], 1.0, 0.0, [K("ii", 1, 2)])
-    for nm, sc, bi in (("i256", 256.0, 0.0), ("ibp", 32768.0, 0.0), ("ibn", -32768.0, 0.0), ("c258", 0.0, 258.0)):
-        aop(nm, 128, T[nm][:], sc, bi, [K(nm)])
+    for nm, sc in UNITS + (("i32", 1.0),):
+        aop(nm, 128, T[nm][:], sc, 0.0, [K(nm)])
+    aop("c258", 128, T.c258[:], 0.0, 258.0, [K("c258")])
+    aop("c25", 128, T.c25[:], 0.0, -CAP / 128, [K("c25")])
+    aop("dq", 128, T.dq[:], col(10), 0.0, [K("dq")], [K("cf", 10, 11)])
     for x in range(2):
         aop("ones", 256, T.ones[:, 256 * x:256 * x + 256], 0.0, 1.0, [K("ones", x, x + 1)])
     vop("ipm", 128, lambda: ts(T.ipm[:], T.cx[:, 0:128], col(8), None, A.is_equal), CX + [K("cf", 8, 9)], [K("ipm")], L)
@@ -255,27 +299,39 @@ def rank_ops(g, core, T, topo, me):
     vop("tri", 256, lambda: V.tensor_tensor(T.tri[:], T.ta[:], T.tb[:], A.mult), [K("ta"), K("tb")], [K("tri")], L)
     vop("di", 8, lambda: ts(T.di[:], T.cx[:, 0:8], col(3), None, A.add), CX + C5, [K("di")], L)
     vop("dj", 8, lambda: ts(T.dj[:], T.di[:], 7, None, A.bitwise_and), [K("di")], [K("dj")], L)
-    vop("df", 8, lambda: V.tensor_copy(T.df[:], T.dj[:]), [K("dj")], [K("df")], L)
-    vop("rst", 448, lambda: V.memset(T.rst[:], 1.0), [], [K("rst")], L)
-    vop("rst0", 8, lambda: V.memset(T.rst[:, 0:896:128], 0.0), [], [K("rst")], L)
-    vop("ee", 8, lambda: V.memset(T.ee[:, 15:1008:144], 0.0), [], [K("ee")], L)
-    vop("zero", 16, lambda: V.memset(win[:, ZCOL:ZCOL + 16], 0.0), [], [K("win", ZCOL, ZCOL + 16)], L)
+    vop("df", 8, lambda: ts(T.df[:], T.dj[:], -3.5, 0.125, A.add, A.mult), [K("dj")], [K("df")], L)
+    vop("top", 456, lambda: V.memset(T.top[:], 256.0), [], [K("top")], L)
+    vop("top0", 8, lambda: V.memset(T.top[:, 0:7 * SEG:SEG], 0.0), [], [K("top")], L)
+    vop("lid", 456, lambda: V.memset(T.lid[:], 0.0), [], [K("lid")], L)
+    vop("hh", 8, lambda: V.memset(T.hh[:, 0:7 * SEG:SEG], 256.0), [], [K("hh")], L)
+    END0 = START[1] + 4 * SL
+    for lo, n in [(x - GAP, GAP) for x in START] + [(END0, 16)]:
+        vop("zero", 64, lambda lo=lo, n=n: V.memset(win[:, lo:lo + n], 0.0), [], [K("win", lo, lo + n)], L)
+    vop("cst", 64, lambda: V.memset(T.cst[:], 0.0), [], [K("cst")], L)
+    for x, c in enumerate(SHIFT):
+        vop("cst", 64, lambda x=x, c=c: V.memset(T.cst[32 * x:32 * x + 1, :], c), [], [K("cst")], L)
+    rise(n0, 40.0)
 
+    n0 = len(ops)
     for d in range(N):
         mm("pg", pb[0][:, 48 * d:48 * d + 16], 0, T.rep[:], T.gh[:, 128 + 16 * d:144 + 16 * d], 16, True, True, [K("rep"), K("gh")])
         mm("pw", pb[0][:, 48 * d + 16:48 * d + 24], 0, T.rep[:], T.kwm[:, d:d + 8], 8, True, True, [K("rep"), K("kwm")])
         mm("ph", pb[0][:, 48 * d + 24:48 * d + 48], 0, T.rep[:], T.gh[:, 16 * d:16 * d + 24], 24, True, True, [K("rep"), K("gh")])
     vop("ps", 384, lambda: V.tensor_copy(T.ps[:], pb[0][:, 0:384]), [], [K("pb0"), K("ps")])
+    rise(n0, 60.0)
     last = send("s_par", [xfer(topo, hands[0], ei, S.hpar, T.ps[:], T.hp[:])], 8, [K("ps")])
     dma("own_par", "s", [(T.pc[:, 2 * me:2 * me + 2, :], T.ps[:, 48 * me:48 * me + 48])], [K("ps")], [K("pc", 0, 1)], 2.0)
     arrive("par", "pa", 7, [K("pc", 1, 2)], 9.5)
 
-    def base(s, r, n=256):
-        return win[:, s * SL + 256 * r:s * SL + 256 * r + n]
+    def at(z, r, q=0):
+        return START[z] + q * SL + 256 * r
 
-    def kb(s, r, n=256, q=0):
-        return K("win", q * 4096 + s * SL + 256 * r, q * 4096 + s * SL + 256 * r + n)
-    for ks in ((1,), (2, 3), (4, 5), (6, 7)):
+    def base(z, r, n=256, q=0):
+        return win[:, at(z, r, q):at(z, r, q) + n]
+
+    def kb(z, r, n=256, q=0):
+        return K("win", at(z, r, q), at(z, r, q) + n)
+    for ks in OUT1:
         last = send("s_1", [xfer(topo, T.cores[me ^ k], share(eo, len(ks), x), S["a1%d" % (k // 2)], T.d1[me ^ k], base(1, me))
                             for x, k in enumerate(ks)], 8, [K("d1")], [last])
     for y in range(2):
@@ -288,95 +344,131 @@ def rank_ops(g, core, T, topo, me):
     for s in (1, 0):
         dma("own%d" % s, "s", [(base(s, me), T["d%d" % s][me])], [K("d%d" % s)], [kb(s, me)], 2.2)
     when = {(1, 0): 6.4, (1, 1): 7.9, (1, 2): 9.5, (1, 3): 11.0, (0, 2): 11.5, (0, 3): 11.6, (0, 0): 13.2, (0, 1): 13.3}
-    for (s, cc), at in when.items():
-        arrive("a%d%d" % (s, cc), "a%d%d" % (s, cc), 8, [kb(s, me ^ k) for k in (2 * cc, 2 * cc + 1) if k], at)
+    for (s, cc), t in when.items():
+        arrive("a%d%d" % (s, cc), "a%d%d" % (s, cc), 8, [kb(s, me ^ k) for k in (2 * cc, 2 * cc + 1) if k], t)
 
     for r in range(N):
-        vop("z", 65, lambda r=r: ts(T.zt[:, 144 * r:144 * r + 129], T.mz[:, 14 - 2 * r:143 - 2 * r], T.pc[:, 2 * r, 16:17], None, A.mult),
-            [K("mz"), K("pc")], [K("zt", r, r + 1)])
-    for nm, up in (("mat", 5.0), ("matp", 0.0)):
-        for b in range(8):
-            o = T.mat[:, :, 16 * b:16 * b + 16] if nm == "mat" else T.matp[:, :, b::8]
-            either(nm, 128, 256, lambda o=o, b=b: ts(o, T.pc[:, :, 0:16], T.bm[:, b:b + 1], None, A.mult),
-                   lambda o=o, b=b: ACT.activation(o, T.pc[:, :, 0:16], F.Identity, scale=T.bm[:, b:b + 1]),
+        vop("z", 65, lambda r=r: ts(T.zt[:, 144 * r:144 * r + 129], T.mz[:, 14 - 2 * r:143 - 2 * r], T.pc[:, 2 * r, 16:17], 0.125,
+                                   A.mult, A.mult), [K("mz"), K("pc")], [K("zt", r, r + 1)])
+        ops[-1]["up"] = UP["a"]
+    for nm, nb in (("mat", 12), ("matp", 8)):
+        for b in range(nb):
+            rows = slice(0, 16) if b < 8 else slice(1, 16, 2)
+            o = T.mat[:, rows, 16 * b:16 * b + 16] if nm == "mat" else T.matp[:, :, b::8]
+            i = T.pc[:, rows, 0:16]
+            n = 128 if b < 8 else 64
+            either(nm, n, 2 * n, lambda o=o, i=i, b=b: ts(o, i, T.bm[:, b % 8:b % 8 + 1], None, A.mult),
+                   lambda o=o, i=i, b=b: ACT.activation(o, i, F.Identity, scale=T.bm[:, b % 8:b % 8 + 1]),
                    [K("bm"), K("pc")], [K(nm, b, b + 1)], L)
-            ops[-1]["up"] = up
+            ops[-1]["up"] = UP[nm]
 
     rb = [0]
 
     def place(cc):
         return (me // 2) ^ cc
 
-    def turn_pe(s, cc, by_dma):
+    def turn_pe(z, cc, nt, banks):
         c = place(cc)
-        for q in range(1, 8):
-            if any(cc in ccs and q in qs for ccs, qs in by_dma):
+        for q in range(1, nt):
+            if any(cc in ccs and q in qs for ccs, qs in BY_DMA[z]) or (q == 4 and cc in BY_POOL[z]):
                 continue
-            b = BANKS[rb[0] % len(BANKS)]
+            b = banks[rb[0] % len(banks)]
             rb[0] += 1
-            mm("rot", pb[b][:], b, T.ii[:, 16 * q:16 * q + 128], base(s, 2 * c, 512), 512, True, True, [K("ii"), kb(s, 2 * c, 512)])
-            o = win[:, q * 4096 + s * SL + 512 * c:q * 4096 + s * SL + 512 * c + 512]
+            mm("rot", pb[b][:], b, T.ii[:, 16 * q:16 * q + 128], base(z, 2 * c, 512), 512, True, True, [K("ii"), kb(z, 2 * c, 512)])
+            ops[-1]["up"] = UP["rot"]
+            o = base(z, 2 * c, 512, q)
             either("evac", 512, 512, lambda o=o, b=b: V.tensor_copy(o, pb[b][:]), lambda o=o, b=b: ACT.activation(o, pb[b][:], F.Copy),
-                   [], [K("pb%d" % b), kb(s, 2 * c, 512, q)])
+                   [], [K("pb%d" % b), kb(z, 2 * c, 512, q)])
+            ops[-1]["up"] = UP["evac"]
 
-    def turn_dma(s, ccs, qs, lat):
+    def turn_dma(z, ccs, qs, after=()):
         c = min(place(cc) for cc in ccs)
         n = 512 * len(ccs)
-        lo = s * SL + 512 * c
+        lo = at(z, 2 * c)
         pairs = []
         for q in qs:
-            o = q * 4096 + lo
+            o = at(z, 2 * c, q)
             pairs.append((win[0:128 - 16 * q, o:o + n], win[16 * q:128, lo:lo + n]))
             pairs.append((win[128 - 16 * q:128, o:o + n], win[0:16 * q, lo:lo + n]))
-        dma("turn", "s", pairs, [kb(s, 2 * c, n)], [kb(s, 2 * c, n, q) for q in qs], lat)
+        return dma("turn", "s", pairs, [kb(z, 2 * c, n)], [kb(z, 2 * c, n, q) for q in qs], 1.8, work=UNIT * len(ccs) * len(qs), after=after)
 
-    def a_part(s, c, first, final):
-        for x in range(4):
-            r, h = 2 * c + x // 2, x % 2
-            lo = s * SL + 256 * r + 128 * h
-            mm("a", pb[7][:, 0:128], 7, T.zt[:, 144 * r + 1 - h:144 * r + 129 - h], win[:, lo:lo + 128], 128, first and x == 0,
-               final and x == 3, [K("zt", r, r + 1), K("win", lo, lo + 128)])
-            ops[-1]["up"] = 2.0
+    def turn_pool(z, cc):
+        c = place(cc)
+        lo, o = at(z, 2 * c), at(z, 2 * c, 4)
+        for x in range(2):
+            gop("pool", 512, lambda x=x: g.affine_select(win[64 * x:64 * x + 64, o:o + 512], win[64 - 64 * x:128 - 64 * x, lo:lo + 512], [[0, 512]],
+                                                         A.is_gt, 0.0, 1, 0), [K("win", o + x, o + 511 + x)], [kb(z, 2 * c, 512)])
 
-    def index():
+    def a_part(z, x, first, final):
+        c = place(WORK[x])
         n0 = len(ops)
-        vop("ai", 128, lambda: V.tensor_copy(T.ai[:], pb[7][:, 0:128]), [], [K("pb7"), K("ai")])
-        vop("wi", 128, lambda: ts(T.wi[:], T.ai[:], 7, None, A.bitwise_and), [K("ai")], [K("wi")])
-        vop("wb", 128, lambda: V.tensor_copy(T.wb[:], T.wi[:]), [K("wi")], [K("wb")])
-        for d in range(7):
-            vop("h", 64, lambda d=d: ts(T.hh[:, 128 * d:128 * d + 128], T.wb[:], T.df[:, d + 1:d + 2], None, A.is_equal),
-                [K("wb"), K("df")], [K("hh", d, d + 1)])
-        vop("scan", 448, lambda: V.tensor_tensor_scan(T.ss[:], T.rst[:], T.hh[:], 0.0, A.mult, A.add), [K("rst"), K("hh")], [K("ss")])
-        mm("off", pb[7][:, 128:135], 7, T.tri[:], T.ss[:, 127:896:128], 7, True, True, [K("tri"), K("ss")])
-        vop("ofs", 8, lambda: ts(T.ofs[:, 0:7], pb[7][:, 128:135], -float(CAP), 0.0, A.add, A.min), [], [K("pb7"), K("ofs")])
-        vop("ui", 128, lambda: ts(T.ui[:], T.ai[:], 3, 0x8FF, A.arith_shift_right, A.bitwise_and), [K("ai")], [K("ui")])
-        vop("a3", 128, lambda: ts(T.a3[:], T.ai[:], 2.0, col(10), A.mult, A.add), [K("ai"), K("cf", 10, 11)], [K("a3")])
-        vop("qi", 128, lambda: ts(T.qi[:], T.a3[:], 0x7000, None, A.bitwise_and), [K("a3")], [K("qi")])
-        vop("qf", 128, lambda: V.tensor_copy(T.qf[:], T.qi[:]), [K("qi")], [K("qf")])
-        fo = pb[3][:, 0:128]
-        mm("f0", fo, 3, T.i256[:], T.wb[:], 128, True, False, [K("i256"), K("wb")])
-        mm("f1", fo, 3, T.ii[:, 0:128], T.qf[:], 128, False, False, [K("ii"), K("qf")])
-        for d in range(7):
-            o = T.ee[:, 144 * d + 16:144 * d + 144]
-            i = T.ss[:, 128 * d:128 * d + 128]
-            ke = K("ee", 144 * d, 144 * d + 144)
-            either("e", 64, 128, lambda o=o, i=i, d=d: ts(o, i, T.ofs[:, d:d + 1], 0.0, A.add, A.max),
-                   lambda o=o, i=i, d=d: ACT.activation(o, i, F.Relu, bias=T.ofs[:, d:d + 1]), [K("ss"), K("ofs")], [ke])
-            mm("fp", fo, 3, T.ibp[:], o, 128, False, False, [K("ibp"), ke])
-            mm("fn", fo, 3, T.ibn[:], T.ee[:, 144 * d + 15:144 * d + 143], 128, False, d == 6, [K("ibn"), ke])
-        vop("tg", 128, lambda: V.tensor_tensor(T.tg[:], fo, T.ui[:], A.add), [K("ui")], [K("pb3"), K("tg")])
-        vop("off", 128, lambda: ts(T.off[:], T.tg[:], float(ZCOL), None, A.min), [K("tg")], [K("off")])
-        for o in ops[n0:]:
-            o["up"] = 3.0
+        if first:
+            mm("a0", pb[6][:, 0:RW], 6, T.cst[:], T.ones[:, 0:RW], RW, True, False, [K("cst"), K("ones")])
+        for y in range(4):
+            r, h = 2 * c + y // 2, y % 2
+            lo = at(z, r) + RW * h
+            mm("a", pb[6][:, 0:RW], 6, T.zt[:, 144 * r + 1 - h:144 * r + 129 - h], win[:, lo:lo + RW], RW, False,
+               final and y == 3, [K("zt", r, r + 1), K("win", lo, lo + RW)])
+        rise(n0, UP["a"])
 
-    for s, ccs, qs in DMA_FIRST:
-        turn_dma(s, ccs, qs, 3.2 * len(ccs))
+    def index(t):
+        n0 = len(ops)
+        kp = K("pb6")
+        xa = pb[6][:, 0:RW]
+        fo = pb[6][:, RW:2 * RW]
+        vop("r3", RW, lambda: ts(T.r3[:], xa, BIG1, BIG1, A.add, A.subtract), [], [kp, K("r3")])
+        vop("r15", RW, lambda: ts(T.r15[:], xa, BIG4096, BIG4096, A.add, A.subtract), [], [kp, K("r15")])
+        vop("wb", RW, lambda: V.tensor_tensor(T.wb[:], xa, T.r3[:], A.subtract), [K("r3")], [kp, K("wb")])
+        vop("yy", RW, lambda: V.tensor_tensor(T.yy[:], xa, T.r15[:], A.subtract), [K("r15")], [kp, K("yy")])
+        for d in (1, 2, 3, 4, 5, 6, 7, 0):
+            o = T.hh[:, SEG * (d - 1) + 1:SEG * d] if d else T.hs[:]
+            x = (4 + d) % 8
+            vop("h", RW // 2, lambda o=o, x=x: ts(o, T.wb[:], T.df[:, x:x + 1], None, A.is_equal), [K("wb"), K("df")],
+                [K("hh", d - 1, d) if d else K("hs")])
+        vop("scan", 7 * SEG // 2, lambda: V.tensor_tensor_scan(T.ss[:, 0:7 * SEG], T.hh[:, 0:7 * SEG], T.top[:, 0:7 * SEG], 0.0, A.add, A.min),
+            [K("top"), K("hh")], [K("ss")])
+        mm("cap", pb[0][:, 0:7], 0, T.c25[:], T.ones[:, 0:7], 7, True, False, [K("c25"), K("ones")])
+        mm("tri", pb[0][:, 0:7], 0, T.tri[:], T.ss[:, RW:7 * SEG:SEG], 7, False, True, [K("tri"), K("ss")])
+        vop("ofs", 8, lambda: ts(T.lid[:, 0:7 * SEG:SEG], pb[0][:, 0:7], -float(RW), 0.0, A.max, A.min), [], [K("pb0"), K("lid")])
+        for lo, hi in ((0, 2), (2, 7)):
+            vop("scan2", (hi - lo) * SEG // 2, lambda a=SEG * lo, b=SEG * hi: V.tensor_tensor_scan(
+                T.cc[:, a:b], T.hh[:, a:b], T.lid[:, a:b], 0.0, A.add, A.min), [K("lid"), K("hh")], [K("cc", lo, hi)])
+        floors = [("lt", "wb", 1.0, KO + 0.5), ("k11", "yy", 1.0 / 256, KO + 7.5), ("k14", "yy", 1.0 / 2048, KO + 0.5), ("k14c", "yy", 1.0 / 2048, col(13))]
+        terms = [("i32", "yy"), ("im1", "wb"), ("i2k", "wb"), ("ii", "lt"), ("im2k", "lt"), ("i18", "k11"), ("is%d" % t, "k14")]
+        step = dict(UNITS)["is%d" % t]
+        tail = GAP + 2047 + 896 + 1024 + 65536 - KO * (1 - 2048 + 1792 + step) + max(0.0, -step)
+        if LISTS[t] == 2:
+            floors.append(("k13c", "yy", 1.0 / 1024, col(14)))
+            terms += [("i24", "k13c"), ("ibn", "k14c")]
+            tail += KO * (65536 - 24576)
+            zero = float(END0)
+        else:
+            terms.append(("im16", "k14c"))
+            tail += KO * 16384
+            zero = float(START[t + 2] - START[t])
+        for nm, src, sc, bi in floors:
+            add(nm, {"a": vd(RW)}, lambda q, nm=nm, src=src, sc=sc, bi=bi: ACT.activation(T[nm][:], T[src][:], F.Identity, bias=bi, scale=sc),
+                [K(src), K("cf", 13, 15)], [K(nm)])
+        for x, (u, v) in enumerate(terms):
+            mm("f", fo, 6, T[u][:, 0:128], T[v][:], 4 * RW if v == "yy" else RW, x == 0, False, [K(u), K(v)])
+        mm("f", fo, 6, T.dq[:], T.ones[:, 0:RW], RW, False, False, [K("dq"), K("ones")])
+        mm("f", fo, 6, T.ibn[:], T.hs[:], RW, False, False, [K("ibn"), K("hs")])
+        for d in range(7):
+            mm("fn", fo, 6, T.ibn[:], T.cc[:, SEG * d + 1:SEG * d + SEG], RW, False, False, [K("ibn"), K("cc", d, d + 1)])
+            mm("fn", fo, 6, T.ibp[:], T.cc[:, SEG * d:SEG * d + RW], RW, False, d == 6, [K("ibp"), K("cc", d, d + 1)])
+        vop("off", RW, lambda: ts(T.off[:, 0:RW], fo, tail, zero, A.add, A.min), [], [kp, K("off", 0, 1)])
+        for x in range(2 * (LISTS[t] - 1)):
+            vop("off", RW, lambda x=x: ts(T.off[64 * x:64 * x + 64, RW:2 * RW], pb[6][64 - 64 * x:128 - 64 * x, RW:2 * RW],
+                                          tail - 32768, zero, A.add, A.min), [], [kp, K("off", 1 + x, 2 + x)])
+        rise(n0, UP["index"])
+
+    early = [turn_dma(0, ccs, qs) for ccs, qs in BY_DMA[0]]
     for s, cc in sorted(when, key=lambda x: when[x]):
         if s == 1:
-            a_part(1, place(cc), cc == 0, cc == 3)
-        if (s, cc) == (1, 3):
-            index()
-        turn_pe(s, cc, [(ccs, qs) for z, ccs, qs in DMA_FIRST if z == s])
+            a_part(1, WORK.index(cc), cc == 0, cc == 3)
+            if cc == 3:
+                index(0)
+        turn_pe(s, cc, 4, BANKS[0])
 
     chunks = [place(cc) for cc in WORK]
 
@@ -388,56 +480,80 @@ def rank_ops(g, core, T, topo, me):
         trs = [xfer(topo, hands[back[k][0]], share(ei, 2, back[k][0]), S["hr%d" % back[k][1]], src(me ^ k), T.hd[8 + back[k][1]]) for k in near]
         trs += [xfer(topo, T.cores[me ^ k], share(eo, len(far), y), S.r1 if land == "l1" else S["r0%d" % k], src(me ^ k), T[land][me])
                 for y, k in enumerate(far)]
-        return send("back", trs, 4 * len(near) + (8 if far else 0), [key], [after])
+        return send("back", trs, 4 * len(near) + (8 if far else 0), [key], [after], 0.5 * UNIT * len(trs))
 
     def lands(back, k):
         return 8 if k in back or (k ^ 1) in back or k == 1 else 4
 
     for t in range(3):
-        s = t % 2
+        nl = LISTS[t]
         mats = T.matp if t == 2 else T.mat
         mk = K("matp") if t == 2 else K("mat")
         unit = T.ipm[:] if t == 2 else T.ii[:, 0:128]
+        lo, hi = START[t] - GAP, END0 + 16 if t == 0 else START[t + 2]
+        W = win[:, lo:hi]
+        kW = K("win", lo, hi)
+        n0 = len(ops)
         for x, c in enumerate(chunks):
             mm("xc", pb[x][:], x, T.c258[:], T.ones[:], 512, True, False, [K("c258"), K("ones")])
-            mm("xo", pb[x][:], x, unit, base(s, 2 * c, 512), 512, False, False, [K("ii"), K("ipm"), kb(s, 2 * c, 512)])
+            mm("xo", pb[x][:], x, unit, base(t, 2 * c, 512), 512, False, False, [K("ipm" if t == 2 else "ii"), kb(t, 2 * c, 512)])
             for y in range(2):
-                mm("xg", pb[x][:, 256 * y:256 * y + 256], x, mats[:, 2 * (2 * c + y), :], base(1 - s, 2 * c + y), 256, False, False,
-                   [mk, kb(1 - s, 2 * c + y)])
-        W = win[:, 0:ZCOL + 16]
-        add("gv", {"v": vd(1600)}, lambda q: V.tensor_copy(T.ref[:, 0:1024], W.indirect(T.off[:, 0:64])), [K("win"), K("off")], [K("ref", 0, 1)])
-        add("ga", {"a": vd(1600)}, lambda q: ACT.activation(T.ref[:, 1024:2048], W.indirect(T.off[:, 64:128]), F.Copy),
-            [K("win"), K("off")], [K("ref", 1, 2)])
-        for x, c in enumerate(chunks):
-            for y in range(4):
-                rp = 4 * c + y
-                mm("xh", pb[x][:, 128 * y:128 * y + 128], x, mats[:, 2 * (rp // 2) + 1, :], T.ref[:, rp::16], 128, False, y == 3, [mk, K("ref")])
+                mm("xg", pb[x][:, 256 * y:256 * y + 256], x, mats[:, 2 * (2 * c + y), 0:128], base(t + 1, 2 * c + y), 256, False, False,
+                   [mk, kb(t + 1, 2 * c + y)])
+        rise(n0, UP["x"])
+        n0 = len(ops)
+        for z in range(nl):
+            for w in range(2):
+                u = 2 * w + z if nl == 2 else w
+                o = T.ref[:, 1024 * u:1024 * u + 1024]
+                i = W.indirect(T.off[:, 64 * u:64 * u + 64])
+                fn = (lambda q, o=o, i=i: V.tensor_copy(o, i)) if w else (lambda q, o=o, i=i: ACT.activation(o, i, F.Copy))
+                add("gather", {"av"[w]: vd(1600)}, fn, [kW, K("off", 1, 3) if u > 1 else K("off", 0, 1)], [K("ref", u, u + 1)])
+        for z in range(nl):
+            for x, c in enumerate(chunks):
+                for w in range(nl):
+                    for y in range(4):
+                        r, n = 2 * c + y // 2, RW // nl
+                        lo = SL * w + 1024 * z
+                        mm("xh", pb[x][:, RW * y + n * z:RW * y + n * z + n], x, mats[:, 2 * r + 1, 64 * w:64 * w + 128],
+                           T.ref[:, lo + 4 * c + y:lo + 16 * n:16], n, False, (z, w, y) == (nl - 1, nl - 1, 3),
+                           [mk, K("ref", 2 * w + z, 2 * w + z + 1) if nl == 2 else K("ref", 0, 2)])
+        rise(n0, UP["wave"])
+        if t == 0:
+            for ccs, qs in LATE:
+                turn_dma(1, ccs, qs, early)
+            for cc in BY_POOL[1]:
+                turn_pool(1, cc)
         for x, c in enumerate(chunks):
             qv = T.qb[:, 512 * x:512 * x + 512]
+            n0 = len(ops)
             if x == 0 and t < 2:
                 vop("m1", 512, lambda x=x, qv=qv: ts(qv, pb[x][:], -127.5, None, A.add), [], [K("pb%d" % x), K("qb", x, x + 1)])
             else:
                 add("m1", {"a": vd(512)}, lambda q, x=x, qv=qv: ACT.activation(qv, pb[x][:], F.Identity, bias=-127.5), [],
                     [K("pb%d" % x), K("qb", x, x + 1)])
-            o = T.fin[:, 512 * c:512 * c + 512] if t == 2 else base(s, 2 * c, 512)
-            ko = K("fin", c, c + 1) if t == 2 else kb(s, 2 * c, 512)
+            o = T.fin[:, 512 * c:512 * c + 512] if t == 2 else base(t + 2, 2 * c, 512)
+            ko = K("fin", c, c + 1) if t == 2 else kb(t + 2, 2 * c, 512)
             vop("m2", 512, lambda x=x, qv=qv, o=o: V.tensor_tensor(o, pb[x][:], qv, A.subtract), [K("qb", x, x + 1)], [K("pb%d" % x), ko])
+            rise(n0, UP["wave"])
             if t == 1:
-                last = give_back(lambda r: base(1, r), ko, "l1", BACK1, x, last)
+                last = give_back(lambda r: base(3, r), ko, "l1", BACK1, x, last)
             if t == 2:
                 last = give_back(lambda r: T.fin[:, 256 * r:256 * r + 256], ko, "l0", BACK0, x, last)
             else:
-                a_part(s, c, x == 0, x == 3)
+                a_part(t + 2, x, x == 0, x == 3)
         if t < 2:
-            for x, (ccs, qs) in enumerate(DMA_WAVE[t]):
-                turn_dma(s, ccs, qs, 3.0 + 0.7 * x)
-            index()
+            for ccs, qs in BY_DMA[t + 2]:
+                turn_dma(t + 2, ccs, qs)
+            for cc in BY_POOL[t + 2]:
+                turn_pool(t + 2, cc)
+            index(t + 1)
             for cc in WORK:
-                turn_pe(s, cc, DMA_WAVE[t])
+                turn_pe(t + 2, cc, 8, BANKS[1])
         if t == 1:
-            dma("own_l1", "s", [(T.l1[me], base(1, me))], [kb(1, me)], [K("l1", 0, 1)], 2.2, pen=0.5)
+            dma("own_l1", "s", [(T.l1[me], base(3, me))], [kb(3, me), K("cc")], [K("l1", 0, 1)], 2.2, pen=0.5)
             arrive("r1", "r1", sum(lands(BACK1, k) for k in range(1, 8)), [K("l1", 1, 2)], 0.0)
-            dma("y1", "s", [(T.y[i::16, SL:2 * SL], T.l1[:, i::16, :]) for i in range(16)], [K("l1")], [], 4.0, pen=1.0)
+            dma("y1", "s", [(T.y[i::16, SL:2 * SL], T.l1[:, i::16, :]) for i in range(16)], [K("l1"), K("off")], [], 4.0, pen=1.0)
     dma("y_own", "a", [(T.y[16 * me:16 * me + 16, 0:SL], T.fin[:, 256 * me:256 * me + 256])], [K("fin")], [], 2.0)
     for x, k in enumerate(STORE0):
         arrive("r0", "r0%d" % k, lands(BACK0, k), [K("l0", k, k + 1)], 0.0)
@@ -460,7 +576,7 @@ def rank_program(g, core, T, topo):
     need = set()
     for n in order:
         for d in ops[n]["deps"]:
-            if not (ops[n]["q"] == "p" and ops[d]["q"] == "p"):
+            if waits(ops[n], d, ops[d], ops[n]["q"]):
                 need.add(d)
     cnt = {}
     seen = {q: {} for q in Q}
@@ -471,7 +587,7 @@ def rank_program(g, core, T, topo):
         want = {}
         for d in o["deps"]:
             p = ops[d]
-            if p["done"] == 0 or (q == "p" and p["q"] == "p"):
+            if p["done"] == 0 or not waits(o, d, p, q) or d in o["after"]:
                 continue
             sem, val = p["done"]
             want[sem] = max(want.get(sem, 0), val)

from concourse.bass import DstId, RemoteDMATransfer
from concourse.mybir import AluOpType, ActivationFunctionType

N = 8
SL = 2048
CAP = 320
GAP = 128
START = (GAP, 2 * GAP + 4 * SL, 3 * GAP + 12 * SL, 4 * GAP + 20 * SL, 5 * GAP + 28 * SL)
LISTS = (2, 1, 1)
RW = 128
SEG = RW + 1
BF = "bfloat16"
SCRATCH = {"win": ("sbuf", [128, START[4]], BF), "off": ("sbuf", [128, 256], "uint16")}
UNITS = (("ibp", 65536.0), ("ibn", -65536.0), ("im1", -1.0), ("i2k", 2048.0), ("im2k", -2048.0), ("i18", 1792.0),
         ("is0", float(START[1] - START[0])), ("is1", float(START[1] - START[2])), ("is2", float(START[3] - START[2])),
         ("i24", 24576.0), ("im16", -16384.0))
for _n, _w in (("ref", 2 * SL), ("qb", SL), ("fin", SL), ("gh", 256), ("kws", 8), ("kwm", 16), ("ps", 384), ("zt", 8 * 144), ("rep", 128),
               ("ii", 256), ("ipm", 128), ("mz", 144), ("tri", 128), ("ta", 128), ("tb", 128), ("dq", 128), ("cst", 128), ("c25", 128),
               ("c258", 128), ("ones", 512), ("top", 912), ("hh", 912), ("ss", 912), ("lid", 912), ("cc", 912), ("wb", 128), ("r15", 128),
               ("hs", 128), ("lt", 128), ("k11", 128), ("k14", 128), ("k13c", 128), ("k14c", 128)) + tuple((u[0], 128) for u in UNITS):
    SCRATCH[_n] = ("sbuf", [128, _w], BF)
for _n, _w in (("hp", 24), ("pc", 24), ("mat", 192), ("matp", 128)):
    SCRATCH[_n] = ("sbuf", [128, 16, _w], BF)
for _n, _w in (("ci", 8), ("di", 8), ("dj", 8)):
    SCRATCH[_n] = ("sbuf", [128, _w], "int32")
for _n, _w in (("cf", 16), ("cx", 144), ("m16", 128), ("keym", 128), ("bm", 16), ("df", 8), ("r3", 128), ("yy", 128), ("i32", 128)):
    SCRATCH[_n] = ("sbuf", [128, _w], "float32")
for _n, _w in (("d0", 8), ("d1", 8), ("hd", 12), ("l0", 8), ("l1", 8)):
    SCRATCH[_n] = ("dram", [_w, 128, 256], BF)
for _b in range(8):
    SCRATCH["pb%d" % _b] = ("psum", [128, 512], "float32")

NDS = 56
SEMAPHORES = (["cv", "ca", "cp", "cg", "ls", "pa", "r1", "hpar", "hfa", "hfb"] + ["hr%d" % k for k in range(4)]
              + ["a%d%d" % (s, c) for s in range(2) for c in range(4)] + ["r0%d" % k for k in range(1, 8)]
              + ["ds%d" % k for k in range(NDS)])

WORK = (2, 3, 1, 0)
BY_DMA = {0: (((2, 3), (1, 2, 3)), ((0, 1), (1,))), 1: (),
          2: (((2,), (1, 2)), ((3,), (1, 2)), ((2, 3), (3, 5, 6)), ((0, 1), (1, 2, 3))),
          3: (((2,), (1, 2)), ((3,), (1, 2)), ((2, 3), (3, 5)), ((0, 1), (1, 2, 3)))}
LATE = (((0, 1), (5, 6, 7)), ((2, 3), (5, 6, 7)))
BY_POOL = {0: (), 1: (0, 1, 2, 3), 2: (2, 3), 3: (2, 3)}
BACK1 = {4: (0, 0), 5: (1, 0), 2: (0, 1), 3: (1, 1)}
BACK0 = {4: (0, 2), 5: (1, 2)}
STORE0 = (6, 7, 2, 3, 4, 5, 1)
OUT1 = ((1,), (2, 3), (4, 5), (6, 7))
FWD0 = ((((4, 5), "hfa"), ((1,), "hfb")), (((6, 7), "hfa"), ((2, 3), "hfb")))
BANKS = ((4, 5, 1, 3), (4, 5, 7, 3, 2))

BIG1 = 1.5 * 2 ** 23
BIG4096 = 1.5 * 2 ** 35
SHIFT = (-2.0 ** 20, 14336.0, 0.0625)
KO = 130

CY = 0.00104
PCY = 0.00052
HOP = 0.1
UNIT = 0.33
LOOK = {"v": 0.25, "a": 0.2, "p": 0.1, "s": 0.0, "g": 0.0}
UP = {"rot": 6.0, "evac": 2.0, "a": 8.0, "index": 3.0, "wave": 6.0, "mat": 8.0, "matp": -3.0, "x": 0.0}


def bits(es):
    return sum(1 << e for e in es)


def hands_of(c, T, topo):
    far = [d for d in T.cores if topo.chip(d) != topo.chip(c)]
    return [h for h in topo.cores_of(c) if topo.die(h) != topo.die(c) and all(topo.may_write(h, d) for d in far)][:2]


def xfer(topo, dst_core, es, sem, src, dst):
    rid, pid, _ = topo.addr(dst_core)
    return RemoteDMATransfer(dst_ids=[DstId(rid=rid, pnc=pid)], dma_engine_mask=bits(es), remote_sem=sem, src=src, dst=dst)


def share(es, n, x):
    w = len(es) // n
    return es[x * w:(x + 1) * w]


def hand_program(g, core, T, topo, me, which):
    S = T.sem
    eo = topo.engines(core, T.cores[me ^ 1])
    sent = 0
    if which == 0:
        g.wait_ge(S.hpar, 8)
        g.remote_dma_fused([xfer(topo, T.cores[me ^ k], eo[k - 1:k], S.pa, T.hp[:, 2 * (me ^ k):2 * (me ^ k) + 2, :],
                                 T.pc[:, 2 * me:2 * me + 2, :]) for k in range(1, 8)], local_sem=S.ls)
        sent += 7
    for ks, sem in FWD0[which]:
        g.wait_ge(S[sem], 2 * len(ks))
        g.remote_dma_fused([xfer(topo, T.cores[me ^ k], share(eo, len(ks), x), S["a0%d" % (k // 2)], T.hd[k],
                                 T.win[:, START[0] + 256 * me:START[0] + 256 * me + 256]) for x, k in enumerate(ks)], local_sem=S.ls)
        sent += 8
    for back, land in ((BACK1, "l1"), (BACK0, "l0")):
        for k in back:
            if back[k][0] == which:
                x = back[k][1]
                g.wait_ge(S["hr%d" % x], 4)
                g.remote_dma_fused([xfer(topo, T.cores[me ^ k], eo, S.r1 if land == "l1" else S["r0%d" % k], T.hd[8 + x],
                                         T[land][me])], local_sem=S.ls)
                sent += 8
    g.wait_ge(S.ls, sent)


def overlap(a, b):
    return a[0] == b[0] and a[1] < b[2] and b[1] < a[2]


def waits(o, d, p, q):
    return not (p["q"] == q and (d in o["soft"] or d in o["after"]))


def lay_out(ops):
    for n, o in enumerate(ops):
        deps = set(o["after"])
        soft = set()
        for m in range(n):
            p = ops[m]
            met = [a for a in o["w"] for b in p["r"] + p["w"] if overlap(a, b)] + [a for a in o["r"] for b in p["w"] if overlap(a, b)]
            if met:
                deps.add(m)
                if all(a[0].startswith("pb") for a in met):
                    soft.add(m)
        o["deps"] = sorted(deps)
        o["soft"] = soft
    succ = [[] for _ in ops]
    for n, o in enumerate(ops):
        for d in o["deps"]:
            succ[d].append(n)
    for n in range(len(ops) - 1, -1, -1):
        o = ops[n]
        own = (min(o["eng"].values()) + o["lat"] + o["work"]) if o["eng"] else 0.0
        o["tail"] = own + max([ops[m]["tail"] + HOP for m in succ[n] if ops[m]["at"] is None] + [0.0])
    free = {}
    miss = [len(o["deps"]) for o in ops]
    ready = []
    order = []
    busy = [0]

    def placed(n):
        for m in succ[n]:
            miss[m] -= 1
            if miss[m] == 0 and ops[m]["at"] is None:
                ready.append(m)
    for n, o in enumerate(ops):
        if o["at"] is None and not o["deps"]:
            ready.append(n)
    for n, o in enumerate(ops):
        if o["at"] is not None:
            o["end"] = o["at"]
            o["q"] = None
            placed(n)
    while ready:
        cand = []
        for n in ready:
            o = ops[n]
            for q, dur in o["eng"].items():
                if q == "v" and busy[0] and len(o["eng"]) > 1:
                    continue
                st = free.get(q, 0.0)
                for d in o["deps"]:
                    if waits(o, d, ops[d], q):
                        st = max(st, ops[d]["end"] + HOP)
                cand.append((st + o["pen"] + 0.3 * (dur - min(o["eng"].values())), n, q, st, dur))
        first = min(cand)
        near = [c for c in cand if c[2] == first[2] and c[0] <= first[0] + LOOK[first[2]]]
        _, n, q, st, dur = max(near, key=lambda c: (ops[c[1]]["tail"] + ops[c[1]]["up"] - 2.0 * (c[0] - first[0]), -c[1]))
        o = ops[n]
        o["q"] = q
        o["st"] = st
        free[q] = st + dur
        o["end"] = st + dur + o["lat"]
        if o["work"]:
            o["end"] = free["dma"] = max(o["end"], free.get("dma", 0.0)) + o["work"]
        ready.remove(n)
        busy[0] += {"r3": 1, "scan2": -0.5}.get(o["name"], 0)
        order.append(n)
        placed(n)
    return order


def rank_ops(g, core, T, topo, me):
    S = T.sem
    A = AluOpType
    F = ActivationFunctionType
    ops = []
    nds = [0]
    sent = [0]
    V, P, ACT = g.vector, g.tensor, g.scalar
    hands = hands_of(core, T, topo)
    eo = topo.engines(core, T.cores[me ^ 1])
    ei = [e for e in topo.engines(core, hands[0]) if e not in eo]

    def add(name, eng, fn, r, w, pen=0.0, lat=0.0, after=(), at=None, done=None, work=0.0):
        ops.append({"name": name, "eng": eng, "fn": fn, "r": list(r), "w": list(w), "pen": pen, "lat": lat, "after": list(after),
                    "at": at, "done": done, "up": 0.0, "work": work})
        return len(ops) - 1

    def rise(n0, up):
        for o in ops[n0:]:
            o["up"] = up

    def K(name, lo=0, hi=1 << 20):
        return (name, lo, hi)

    def vd(n):
        return 0.06 + max(64, n) * CY

    def vop(name, n, fn, r, w, pen=0.0):
        return add(name, {"v": vd(n)}, lambda q: fn(), r, w, pen)

    def either(name, nv, na, fv, fa, r, w, pen=0.0):
        return add(name, {"v": vd(nv), "a": vd(na)}, lambda q: fv() if q == "v" else fa(), r, w, pen)

    def mm(name, out, bank, lhsT, rhs, n, start, stop, r, pen=0.0):
        return add(name, {"p": 0.01 + max(64, n) * PCY}, lambda q: P.matmul(out, lhsT, rhs, start, stop), r, [K("pb%d" % bank)], pen, 0.05)

    def dma(name, q, pairs, r, w, lat, pen=0.0, work=0.0, after=()):
        sem = "ds%d" % nds[0]
        nds[0] += 1
        Q = {"s": g.sync, "a": g.scalar}[q]

        def fn(_q):
            for o, i in pairs:
                Q.dma_start(o, i).then_inc(S[sem], 16)
        return add(name, {q: 0.08 * len(pairs)}, fn, r, w, pen, lat, done=(sem, 16 * len(pairs)), work=work, after=after)

    def send(name, trs, cnt, r, after=(), work=0.0):
        sent[0] += cnt
        n = add(name, {"g": 0.6}, lambda q: g.remote_dma_fused(trs, local_sem=S.ls), r, [], after=after, done=0, work=work)
        ops[n]["up"] = 30.0
        return n

    def arrive(name, sem, cnt, w, at):
        return add(name, {}, None, [], w, at=at, done=(sem, cnt))

    def ts(out, in0, s1, s2, op0, op1=None):
        if op1 is None:
            return V.tensor_scalar(out, in0, s1, None, op0)
        return V.tensor_scalar(out, in0, s1, s2, op0, op1)

    pb = [T["pb%d" % b] for b in range(8)]
    win = T.win

    dma("ld_gm", "s", [(T.gh[:, 128:256], T.gm[:]), (T.kws[:, 0:1], T.kw[:])], [], [K("gh", 128, 256), K("kws")], 2.0)
    dma("ld_hm", "a", [(T.gh[:, 0:128], T.hm[:])], [], [K("gh", 0, 128)], 2.0)
    for s, lat in ((1, 3.4), (0, 4.6)):
        d = T["d%d" % s]
        for x, q in enumerate("sa"):
            dma("stage%d%s" % (s, q), q, [(d[:, i::16, :], T.m[i::16, s * SL:(s + 1) * SL]) for i in range(x, 16, 2)], [],
                [K("d%d" % s, x, x + 1)], lat, pen=0.01)

    def gop(name, n, fn, w, r=()):
        return add(name, {"g": 0.16 + 2 * n * CY}, lambda q: fn(), r, w)
    gop("io_p", 1, lambda: g.iota(T.ci[:, 0:1], [[0, 1]], 0, 1), [K("ci", 0, 1)])
    gop("io_m16", 128, lambda: g.iota(T.m16[:], [[0, 8], [1, 16]], 0, 0, allow_small_or_imprecise_dtypes=True), [K("m16")])
    gop("io_cx", 144, lambda: g.iota(T.cx[:], [[1, 144]], 0, 0, allow_small_or_imprecise_dtypes=True), [K("cx")])
    gop("io_key", 128, lambda: g.iota(T.keym[:], [[2, 8], [64, 8], [1, 2]], 0, 0, allow_small_or_imprecise_dtypes=True), [K("keym")])
    p0 = T.ci[:, 0:1]
    for x, (sh, mk) in enumerate(((0, 15), (4, 7), (1, 7), (0, 1))):
        vop("ci%d" % x, 1, lambda x=x, sh=sh, mk=mk: ts(T.ci[:, x + 1:x + 2], p0, sh, mk, A.arith_shift_right, A.bitwise_and),
            [K("ci", 0, 1)], [K("ci", x + 1, x + 2)])
    vop("cf", 5, lambda: V.tensor_copy(T.cf[:, 0:5], T.ci[:, 0:5]), [K("ci")], [K("cf", 0, 5)])

    def col(x):
        return T.cf[:, x:x + 1]
    C5 = [K("cf", 0, 5)]
    CX = [K("cx")]
    L = 0.3
    vop("rep", 128, lambda: ts(T.rep[:], T.m16[:], col(1), None, A.is_equal), C5 + [K("m16")], [K("rep")])
    vop("bm", 16, lambda: ts(T.bm[:], T.cx[:, 0:16], col(2), None, A.is_equal), CX + C5, [K("bm")])
    vop("kwm", 16, lambda: ts(T.kwm[:], T.bm[:], T.kws[:, 0:1], None, A.mult), [K("bm"), K("kws")], [K("kwm")])
    rise(0, 60.0)
    n0 = len(ops)
    for nm, x, a, s1, s2, rd in (("k1", 5, 3, 64.0, col(4), []), ("key", 6, 2, 2.0, col(5), [K("cf", 5, 6)]),
                                 ("key32", 7, 6, 1.0, 32.0, [K("cf", 6, 7)]), ("iperm", 8, 1, 8.0, col(2), []),
                                 ("mzc", 9, 2, 16.0, 15.0, []), ("qcol", 10, 2, -2048.0, 16384.0, []), ("q14", 13, 2, -0.125, KO + 1.5, []),
                                 ("q13", 14, 2, -0.25, KO + 3.5, [])):
        vop(nm, 1, lambda x=x, a=a, s1=s1, s2=s2: ts(col(x), col(a), s1, s2, A.mult, A.add), C5 + rd, [K("cf", x, x + 1)], L)
    vop("ii", 128, lambda: ts(T.ii[:, 0:128], T.cx[:, 0:128], col(0), None, A.is_equal), C5 + CX, [K("ii", 0, 1)], L)

    def aop(name, n, o, sc, bi, w, r=()):
        add(name, {"a": vd(n)}, lambda q: ACT.activation(o, T.ii[:, 0:n], F.Identity, bias=bi, scale=sc), [K("ii", 0, 1 + n // 256)] + list(r), w)
    aop("ii2", 128, T.ii[:, 128:256], 1.0, 0.0, [K("ii", 1, 2)])
    for nm, sc in UNITS + (("i32", 1.0),):
        aop(nm, 128, T[nm][:], sc, 0.0, [K(nm)])
    aop("c258", 128, T.c258[:], 0.0, 258.0, [K("c258")])
    aop("c25", 128, T.c25[:], 0.0, -CAP / 128, [K("c25")])
    aop("dq", 128, T.dq[:], col(10), 0.0, [K("dq")], [K("cf", 10, 11)])
    for x in range(2):
        aop("ones", 256, T.ones[:, 256 * x:256 * x + 256], 0.0, 1.0, [K("ones", x, x + 1)])
    vop("ipm", 128, lambda: ts(T.ipm[:], T.cx[:, 0:128], col(8), None, A.is_equal), CX + [K("cf", 8, 9)], [K("ipm")], L)
    vop("mz", 144, lambda: ts(T.mz[:], T.cx[:], col(9), None, A.is_equal), CX + [K("cf", 9, 10)], [K("mz")], L)
    vop("ta", 128, lambda: ts(T.ta[:], T.keym[:], col(6), None, A.is_gt), [K("keym"), K("cf", 6, 7)], [K("ta")], L)
    vop("tb", 128, lambda: ts(T.tb[:], T.keym[:], col(7), None, A.is_lt), [K("keym"), K("cf", 7, 8)], [K("tb")], L)
    vop("tri", 256, lambda: V.tensor_tensor(T.tri[:], T.ta[:], T.tb[:], A.mult), [K("ta"), K("tb")], [K("tri")], L)
    vop("di", 8, lambda: ts(T.di[:], T.cx[:, 0:8], col(3), None, A.add), CX + C5, [K("di")], L)
    vop("dj", 8, lambda: ts(T.dj[:], T.di[:], 7, None, A.bitwise_and), [K("di")], [K("dj")], L)
    vop("df", 8, lambda: ts(T.df[:], T.dj[:], -3.5, 0.125, A.add, A.mult), [K("dj")], [K("df")], L)
    vop("top", 456, lambda: V.memset(T.top[:], 256.0), [], [K("top")], L)
    vop("top0", 8, lambda: V.memset(T.top[:, 0:7 * SEG:SEG], 0.0), [], [K("top")], L)
    vop("lid", 456, lambda: V.memset(T.lid[:], 0.0), [], [K("lid")], L)
    vop("hh", 8, lambda: V.memset(T.hh[:, 0:7 * SEG:SEG], 256.0), [], [K("hh")], L)
    END0 = START[1] + 4 * SL
    for lo, n in [(x - GAP, GAP) for x in START] + [(END0, 16)]:
        vop("zero", 64, lambda lo=lo, n=n: V.memset(win[:, lo:lo + n], 0.0), [], [K("win", lo, lo + n)], L)
    vop("cst", 64, lambda: V.memset(T.cst[:], 0.0), [], [K("cst")], L)
    for x, c in enumerate(SHIFT):
        vop("cst", 64, lambda x=x, c=c: V.memset(T.cst[32 * x:32 * x + 1, :], c), [], [K("cst")], L)
    rise(n0, 40.0)

    n0 = len(ops)
    for d in range(N):
        mm("pg", pb[0][:, 48 * d:48 * d + 16], 0, T.rep[:], T.gh[:, 128 + 16 * d:144 + 16 * d], 16, True, True, [K("rep"), K("gh")])
        mm("pw", pb[0][:, 48 * d + 16:48 * d + 24], 0, T.rep[:], T.kwm[:, d:d + 8], 8, True, True, [K("rep"), K("kwm")])
        mm("ph", pb[0][:, 48 * d + 24:48 * d + 48], 0, T.rep[:], T.gh[:, 16 * d:16 * d + 24], 24, True, True, [K("rep"), K("gh")])
    vop("ps", 384, lambda: V.tensor_copy(T.ps[:], pb[0][:, 0:384]), [], [K("pb0"), K("ps")])
    rise(n0, 60.0)
    last = send("s_par", [xfer(topo, hands[0], ei, S.hpar, T.ps[:], T.hp[:])], 8, [K("ps")])
    dma("own_par", "s", [(T.pc[:, 2 * me:2 * me + 2, :], T.ps[:, 48 * me:48 * me + 48])], [K("ps")], [K("pc", 0, 1)], 2.0)
    arrive("par", "pa", 7, [K("pc", 1, 2)], 9.5)

    def at(z, r, q=0):
        return START[z] + q * SL + 256 * r

    def base(z, r, n=256, q=0):
        return win[:, at(z, r, q):at(z, r, q) + n]

    def kb(z, r, n=256, q=0):
        return K("win", at(z, r, q), at(z, r, q) + n)
    for ks in OUT1:
        last = send("s_1", [xfer(topo, T.cores[me ^ k], share(eo, len(ks), x), S["a1%d" % (k // 2)], T.d1[me ^ k], base(1, me))
                            for x, k in enumerate(ks)], 8, [K("d1")], [last])
    for y in range(2):
        trs = []
        for h in range(2):
            ks, sem = FWD0[h][y]
            for k in ks:
                trs.append(xfer(topo, hands[h], share(ei, 4, len(trs)), S[sem], T.d0[me ^ k], T.hd[k]))
        last = send("s_0", trs, 2 * len(trs), [K("d0")], [last])
    for s in (1, 0):
        dma("own%d" % s, "s", [(base(s, me), T["d%d" % s][me])], [K("d%d" % s)], [kb(s, me)], 2.2)
    when = {(1, 0): 6.4, (1, 1): 7.9, (1, 2): 9.5, (1, 3): 11.0, (0, 2): 11.5, (0, 3): 11.6, (0, 0): 13.2, (0, 1): 13.3}
    for (s, cc), t in when.items():
        arrive("a%d%d" % (s, cc), "a%d%d" % (s, cc), 8, [kb(s, me ^ k) for k in (2 * cc, 2 * cc + 1) if k], t)

    for r in range(N):
        vop("z", 65, lambda r=r: ts(T.zt[:, 144 * r:144 * r + 129], T.mz[:, 14 - 2 * r:143 - 2 * r], T.pc[:, 2 * r, 16:17], 0.125,
                                   A.mult, A.mult), [K("mz"), K("pc")], [K("zt", r, r + 1)])
        ops[-1]["up"] = UP["a"]
    for nm, nb in (("mat", 12), ("matp", 8)):
        for b in range(nb):
            rows = slice(0, 16) if b < 8 else slice(1, 16, 2)
            o = T.mat[:, rows, 16 * b:16 * b + 16] if nm == "mat" else T.matp[:, :, b::8]
            i = T.pc[:, rows, 0:16]
            n = 128 if b < 8 else 64
            either(nm, n, 2 * n, lambda o=o, i=i, b=b: ts(o, i, T.bm[:, b % 8:b % 8 + 1], None, A.mult),
                   lambda o=o, i=i, b=b: ACT.activation(o, i, F.Identity, scale=T.bm[:, b % 8:b % 8 + 1]),
                   [K("bm"), K("pc")], [K(nm, b, b + 1)], L)
            ops[-1]["up"] = UP[nm]

    rb = [0]

    def place(cc):
        return (me // 2) ^ cc

    def turn_pe(z, cc, nt, banks):
        c = place(cc)
        for q in range(1, nt):
            if any(cc in ccs and q in qs for ccs, qs in BY_DMA[z]) or (q == 4 and cc in BY_POOL[z]):
                continue
            b = banks[rb[0] % len(banks)]
            rb[0] += 1
            mm("rot", pb[b][:], b, T.ii[:, 16 * q:16 * q + 128], base(z, 2 * c, 512), 512, True, True, [K("ii"), kb(z, 2 * c, 512)])
            ops[-1]["up"] = UP["rot"]
            o = base(z, 2 * c, 512, q)
            either("evac", 512, 512, lambda o=o, b=b: V.tensor_copy(o, pb[b][:]), lambda o=o, b=b: ACT.activation(o, pb[b][:], F.Copy),
                   [], [K("pb%d" % b), kb(z, 2 * c, 512, q)])
            ops[-1]["up"] = UP["evac"]

    def turn_dma(z, ccs, qs, after=()):
        c = min(place(cc) for cc in ccs)
        n = 512 * len(ccs)
        lo = at(z, 2 * c)
        pairs = []
        for q in qs:
            o = at(z, 2 * c, q)
            pairs.append((win[0:128 - 16 * q, o:o + n], win[16 * q:128, lo:lo + n]))
            pairs.append((win[128 - 16 * q:128, o:o + n], win[0:16 * q, lo:lo + n]))
        return dma("turn", "s", pairs, [kb(z, 2 * c, n)], [kb(z, 2 * c, n, q) for q in qs], 1.8, work=UNIT * len(ccs) * len(qs), after=after)

    def turn_pool(z, cc):
        c = place(cc)
        lo, o = at(z, 2 * c), at(z, 2 * c, 4)
        for x in range(2):
            gop("pool", 512, lambda x=x: g.affine_select(win[64 * x:64 * x + 64, o:o + 512], win[64 - 64 * x:128 - 64 * x, lo:lo + 512], [[0, 512]],
                                                         A.is_gt, 0.0, 1, 0), [K("win", o + x, o + 511 + x)], [kb(z, 2 * c, 512)])

    def a_part(z, x, first, final):
        c = place(WORK[x])
        n0 = len(ops)
        if first:
            mm("a0", pb[6][:, 0:RW], 6, T.cst[:], T.ones[:, 0:RW], RW, True, False, [K("cst"), K("ones")])
        for y in range(4):
            r, h = 2 * c + y // 2, y % 2
            lo = at(z, r) + RW * h
            mm("a", pb[6][:, 0:RW], 6, T.zt[:, 144 * r + 1 - h:144 * r + 129 - h], win[:, lo:lo + RW], RW, False,
               final and y == 3, [K("zt", r, r + 1), K("win", lo, lo + RW)])
        rise(n0, UP["a"])

    def index(t):
        n0 = len(ops)
        kp = K("pb6")
        xa = pb[6][:, 0:RW]
        fo = pb[6][:, RW:2 * RW]
        vop("r3", RW, lambda: ts(T.r3[:], xa, BIG1, BIG1, A.add, A.subtract), [], [kp, K("r3")])
        vop("r15", RW, lambda: ts(T.r15[:], xa, BIG4096, BIG4096, A.add, A.subtract), [], [kp, K("r15")])
        vop("wb", RW, lambda: V.tensor_tensor(T.wb[:], xa, T.r3[:], A.subtract), [K("r3")], [kp, K("wb")])
        vop("yy", RW, lambda: V.tensor_tensor(T.yy[:], xa, T.r15[:], A.subtract), [K("r15")], [kp, K("yy")])
        for d in (1, 2, 3, 4, 5, 6, 7, 0):
            o = T.hh[:, SEG * (d - 1) + 1:SEG * d] if d else T.hs[:]
            x = (4 + d) % 8
            vop("h", RW // 2, lambda o=o, x=x: ts(o, T.wb[:], T.df[:, x:x + 1], None, A.is_equal), [K("wb"), K("df")],
                [K("hh", d - 1, d) if d else K("hs")])
        vop("scan", 7 * SEG // 2, lambda: V.tensor_tensor_scan(T.ss[:, 0:7 * SEG], T.hh[:, 0:7 * SEG], T.top[:, 0:7 * SEG], 0.0, A.add, A.min),
            [K("top"), K("hh")], [K("ss")])
        mm("cap", pb[0][:, 0:7], 0, T.c25[:], T.ones[:, 0:7], 7, True, False, [K("c25"), K("ones")])
        mm("tri", pb[0][:, 0:7], 0, T.tri[:], T.ss[:, RW:7 * SEG:SEG], 7, False, True, [K("tri"), K("ss")])
        vop("ofs", 8, lambda: ts(T.lid[:, 0:7 * SEG:SEG], pb[0][:, 0:7], -float(RW), 0.0, A.max, A.min), [], [K("pb0"), K("lid")])
        for lo, hi in ((0, 2), (2, 7)):
            vop("scan2", (hi - lo) * SEG // 2, lambda a=SEG * lo, b=SEG * hi: V.tensor_tensor_scan(
                T.cc[:, a:b], T.hh[:, a:b], T.lid[:, a:b], 0.0, A.add, A.min), [K("lid"), K("hh")], [K("cc", lo, hi)])
        floors = [("lt", "wb", 1.0, KO + 0.5), ("k11", "yy", 1.0 / 256, KO + 7.5), ("k14", "yy", 1.0 / 2048, KO + 0.5), ("k14c", "yy", 1.0 / 2048, col(13))]
        terms = [("i32", "yy"), ("im1", "wb"), ("i2k", "wb"), ("ii", "lt"), ("im2k", "lt"), ("i18", "k11"), ("is%d" % t, "k14")]
        step = dict(UNITS)["is%d" % t]
        tail = GAP + 2047 + 896 + 1024 + 65536 - KO * (1 - 2048 + 1792 + step) + max(0.0, -step)
        if LISTS[t] == 2:
            floors.append(("k13c", "yy", 1.0 / 1024, col(14)))
            terms += [("i24", "k13c"), ("ibn", "k14c")]
            tail += KO * (65536 - 24576)
            zero = float(END0)
        else:
            terms.append(("im16", "k14c"))
            tail += KO * 16384
            zero = float(START[t + 2] - START[t])
        for nm, src, sc, bi in floors:
            add(nm, {"a": vd(RW)}, lambda q, nm=nm, src=src, sc=sc, bi=bi: ACT.activation(T[nm][:], T[src][:], F.Identity, bias=bi, scale=sc),
                [K(src), K("cf", 13, 15)], [K(nm)])
        for x, (u, v) in enumerate(terms):
            mm("f", fo, 6, T[u][:, 0:128], T[v][:], 4 * RW if v == "yy" else RW, x == 0, False, [K(u), K(v)])
        mm("f", fo, 6, T.dq[:], T.ones[:, 0:RW], RW, False, False, [K("dq"), K("ones")])
        mm("f", fo, 6, T.ibn[:], T.hs[:], RW, False, False, [K("ibn"), K("hs")])
        for d in range(7):
            mm("fn", fo, 6, T.ibn[:], T.cc[:, SEG * d + 1:SEG * d + SEG], RW, False, False, [K("ibn"), K("cc", d, d + 1)])
            mm("fn", fo, 6, T.ibp[:], T.cc[:, SEG * d:SEG * d + RW], RW, False, d == 6, [K("ibp"), K("cc", d, d + 1)])
        vop("off", RW, lambda: ts(T.off[:, 0:RW], fo, tail, zero, A.add, A.min), [], [kp, K("off", 0, 1)])
        for x in range(2 * (LISTS[t] - 1)):
            vop("off", RW, lambda x=x: ts(T.off[64 * x:64 * x + 64, RW:2 * RW], pb[6][64 - 64 * x:128 - 64 * x, RW:2 * RW],
                                          tail - 32768, zero, A.add, A.min), [], [kp, K("off", 1 + x, 2 + x)])
        rise(n0, UP["index"])

    early = [turn_dma(0, ccs, qs) for ccs, qs in BY_DMA[0]]
    for s, cc in sorted(when, key=lambda x: when[x]):
        if s == 1:
            a_part(1, WORK.index(cc), cc == 0, cc == 3)
            if cc == 3:
                index(0)
        turn_pe(s, cc, 4, BANKS[0])

    chunks = [place(cc) for cc in WORK]

    def give_back(src, key, land, back, x, after):
        cc = WORK[x]
        ks = [k for k in (2 * cc, 2 * cc + 1) if k]
        near = [k for k in ks if k in back]
        far = [k for k in ks if k not in back]
        trs = [xfer(topo, hands[back[k][0]], share(ei, 2, back[k][0]), S["hr%d" % back[k][1]], src(me ^ k), T.hd[8 + back[k][1]]) for k in near]
        trs += [xfer(topo, T.cores[me ^ k], share(eo, len(far), y), S.r1 if land == "l1" else S["r0%d" % k], src(me ^ k), T[land][me])
                for y, k in enumerate(far)]
        return send("back", trs, 4 * len(near) + (8 if far else 0), [key], [after], 0.5 * UNIT * len(trs))

    def lands(back, k):
        return 8 if k in back or (k ^ 1) in back or k == 1 else 4

    for t in range(3):
        nl = LISTS[t]
        mats = T.matp if t == 2 else T.mat
        mk = K("matp") if t == 2 else K("mat")
        unit = T.ipm[:] if t == 2 else T.ii[:, 0:128]
        lo, hi = START[t] - GAP, END0 + 16 if t == 0 else START[t + 2]
        W = win[:, lo:hi]
        kW = K("win", lo, hi)
        n0 = len(ops)
        for x, c in enumerate(chunks):
            mm("xc", pb[x][:], x, T.c258[:], T.ones[:], 512, True, False, [K("c258"), K("ones")])
            mm("xo", pb[x][:], x, unit, base(t, 2 * c, 512), 512, False, False, [K("ipm" if t == 2 else "ii"), kb(t, 2 * c, 512)])
            for y in range(2):
                mm("xg", pb[x][:, 256 * y:256 * y + 256], x, mats[:, 2 * (2 * c + y), 0:128], base(t + 1, 2 * c + y), 256, False, False,
                   [mk, kb(t + 1, 2 * c + y)])
        rise(n0, UP["x"])
        n0 = len(ops)
        for z in range(nl):
            for w in range(2):
                u = 2 * w + z if nl == 2 else w
                o = T.ref[:, 1024 * u:1024 * u + 1024]
                i = W.indirect(T.off[:, 64 * u:64 * u + 64])
                fn = (lambda q, o=o, i=i: V.tensor_copy(o, i)) if w else (lambda q, o=o, i=i: ACT.activation(o, i, F.Copy))
                add("gather", {"av"[w]: vd(1600)}, fn, [kW, K("off", 1, 3) if u > 1 else K("off", 0, 1)], [K("ref", u, u + 1)])
        for z in range(nl):
            for x, c in enumerate(chunks):
                for w in range(nl):
                    for y in range(4):
                        r, n = 2 * c + y // 2, RW // nl
                        lo = SL * w + 1024 * z
                        mm("xh", pb[x][:, RW * y + n * z:RW * y + n * z + n], x, mats[:, 2 * r + 1, 64 * w:64 * w + 128],
                           T.ref[:, lo + 4 * c + y:lo + 16 * n:16], n, False, (z, w, y) == (nl - 1, nl - 1, 3),
                           [mk, K("ref", 2 * w + z, 2 * w + z + 1) if nl == 2 else K("ref", 0, 2)])
        rise(n0, UP["wave"])
        if t == 0:
            for ccs, qs in LATE:
                turn_dma(1, ccs, qs, early)
            for cc in BY_POOL[1]:
                turn_pool(1, cc)
        for x, c in enumerate(chunks):
            qv = T.qb[:, 512 * x:512 * x + 512]
            n0 = len(ops)
            if x == 0 and t < 2:
                vop("m1", 512, lambda x=x, qv=qv: ts(qv, pb[x][:], -127.5, None, A.add), [], [K("pb%d" % x), K("qb", x, x + 1)])
            else:
                add("m1", {"a": vd(512)}, lambda q, x=x, qv=qv: ACT.activation(qv, pb[x][:], F.Identity, bias=-127.5), [],
                    [K("pb%d" % x), K("qb", x, x + 1)])
            o = T.fin[:, 512 * c:512 * c + 512] if t == 2 else base(t + 2, 2 * c, 512)
            ko = K("fin", c, c + 1) if t == 2 else kb(t + 2, 2 * c, 512)
            vop("m2", 512, lambda x=x, qv=qv, o=o: V.tensor_tensor(o, pb[x][:], qv, A.subtract), [K("qb", x, x + 1)], [K("pb%d" % x), ko])
            rise(n0, UP["wave"])
            if t == 1:
                last = give_back(lambda r: base(3, r), ko, "l1", BACK1, x, last)
            if t == 2:
                last = give_back(lambda r: T.fin[:, 256 * r:256 * r + 256], ko, "l0", BACK0, x, last)
            else:
                a_part(t + 2, x, x == 0, x == 3)
        if t < 2:
            for ccs, qs in BY_DMA[t + 2]:
                turn_dma(t + 2, ccs, qs)
            for cc in BY_POOL[t + 2]:
                turn_pool(t + 2, cc)
            index(t + 1)
            for cc in WORK:
                turn_pe(t + 2, cc, 8, BANKS[1])
        if t == 1:
            dma("own_l1", "s", [(T.l1[me], base(3, me))], [kb(3, me), K("cc")], [K("l1", 0, 1)], 2.2, pen=0.5)
            arrive("r1", "r1", sum(lands(BACK1, k) for k in range(1, 8)), [K("l1", 1, 2)], 0.0)
            dma("y1", "s", [(T.y[i::16, SL:2 * SL], T.l1[:, i::16, :]) for i in range(16)], [K("l1"), K("off")], [], 4.0, pen=1.0)
    dma("y_own", "a", [(T.y[16 * me:16 * me + 16, 0:SL], T.fin[:, 256 * me:256 * me + 256])], [K("fin")], [], 2.0)
    for x, k in enumerate(STORE0):
        arrive("r0", "r0%d" % k, lands(BACK0, k), [K("l0", k, k + 1)], 0.0)
        dma("y0", "sa"[x % 2], [(T.y[16 * (me ^ k):16 * (me ^ k) + 16, 0:SL], T.l0[me ^ k])], [K("l0", k, k + 1), K("fin")], [], 2.0,
            pen=0.1 + 0.01 * x)
    return ops, sent[0]


def rank_program(g, core, T, topo):
    me = T.rank_of(core)
    if me is None:
        for c in topo.cores_of(core):
            r = T.rank_of(c)
            if r is not None and core in hands_of(c, T, topo):
                hand_program(g, core, T, topo, r, hands_of(c, T, topo).index(core))
        return
    ops, sent = rank_ops(g, core, T, topo, me)
    order = lay_out(ops)
    Q = {"v": g.vector, "a": g.scalar, "p": g.tensor, "s": g.sync, "g": g}
    need = set()
    for n in order:
        for d in ops[n]["deps"]:
            if waits(ops[n], d, ops[d], ops[n]["q"]):
                need.add(d)
    cnt = {}
    seen = {q: {} for q in Q}
    total = {}
    for n in order:
        o = ops[n]
        q = o["q"]
        want = {}
        for d in o["deps"]:
            p = ops[d]
            if p["done"] == 0 or not waits(o, d, p, q) or d in o["after"]:
                continue
            sem, val = p["done"]
            want[sem] = max(want.get(sem, 0), val)
        for sem, val in want.items():
            if seen[q].get(sem, 0) < val:
                Q[q].wait_ge(T.sem[sem], val)
                seen[q][sem] = val
        ins = o["fn"](q)
        if o["done"] is None:
            if n in need:
                cnt[q] = cnt.get(q, 0) + 1
                o["done"] = ("c" + q, cnt[q])
                ins.then_inc(T.sem["c" + q], 1)
            else:
                o["done"] = 0
        if o["done"] != 0:
            total[o["done"][0]] = o["done"][1]
    for sem, val in total.items():
        if not any(seen[q].get(sem, 0) >= val for q in Q):
            g.wait_ge(T.sem[sem], val)
    g.wait_ge(T.sem.ls, sent)
